import numpy as np, ml_dtypes
CORES = [10,34,74,98]
N = 4
BF = ml_dtypes.bfloat16
V, D, L, RO, HOP = 3072, 12, 256, 4, 2
def meet(rng, n, rest):
    p = np.argsort(rng.random((N, 8, n, V)), axis=-1); h = np.zeros_like(p)
    np.put_along_axis(h, p[..., 0::2], p[..., 1::2], 3); np.put_along_axis(h, p[..., 1::2], p[..., 0::2], 3)
    o = np.concatenate([h, rest], axis=2)
    return np.ascontiguousarray(np.take_along_axis(o, np.argsort(rng.random(o.shape), axis=2), 2))
def court(rng, lo, hi):
    c = rng.integers(0, V, (N, 8, V))
    for r in range(N):
        for g in range(8):
            h = int(rng.integers(3, 10)); chief = rng.permutation(V)[:h]; w = np.add.accumulate(np.exp2(-(0.1 + rng.random()) * np.arange(h)))
            j = np.minimum(np.searchsorted(w, rng.random(V) * w[-1], side="right"), h - 1)
            c[r, g] = np.where(rng.random(V) < lo + (hi - lo) * rng.random(), chief[j], c[r, g])
    return c
def hubs(rng, og, n):
    z = rng.permutation(V)[:RO * n]; vv = np.concatenate([D * rng.permutation(L)[:16 * n] + t for t in range(RO)]).reshape(RO * n, 16)
    og[rng.integers(0, 16, vv.shape), vv] = z[:, None]; og[:, z] = vv.T
    return z
def pack(o, x, c):
    return {"hol": np.ascontiguousarray(o.reshape(N, 128, V)).astype(np.int32), "sha": np.ascontiguousarray(x.reshape(N, 128, V)).astype(np.float32).astype(BF), "ctl": c.astype(np.int32)}
def setup_inputs(rng):
    o = meet(rng, 8, rng.integers(0, V, (N, 8, 8, V))); c = court(rng, 0.85, 0.95); x = rng.integers(0, 16, (N, 8, 16, V))
    for r in range(N):
        for g in range(8): hubs(rng, o[r, g], 2)
    return pack(o, x, c)
def setup_inputs_spread(rng):
    e = rng.integers(1, 7, (N, 8, 1, 1)); o = meet(rng, 8, np.minimum((V * rng.random((N, 8, 8, V)) ** e).astype(np.int64), V - 1))
    c = court(rng, 0.5, 1.0); q = np.minimum((V * rng.random((N, 8, V)) ** rng.integers(1, 9, (N, 8, 1))).astype(np.int64), V - 1)
    c = np.where(rng.random((N, 8, V)) < 0.15, q, c)
    x = np.minimum((rng.random((N, 8, 16, V)) * rng.choice(np.array([1, 2, 3, 6, 11, 16]), (N, 8, 1, V))).astype(np.int64), 15)
    return pack(o, x, c)
def setup_inputs_ends(rng):
    top = V - 1; p = rng.choice(np.array([0.15, 0.5, 0.85]), (N, 8, 1, V)); odd = np.arange(16) % 2
    o = meet(rng, 6, np.where(rng.random((N, 8, 10, V)) < p, top, 0)); c = top * rng.integers(0, 2, (N, 8, V)); kind = rng.random((N, 8, 1, V))
    x = 15 * np.where(kind < 0.45, 1, np.where(kind < 0.55, 0, rng.integers(0, 2, (N, 8, 16, V))))
    for r in range(N):
        for g in range(8):
            og, xg, cg = o[r, g], x[r, g], c[r, g]
            if g % 4 == 1: cg[0] = top; cg[top] = 0
            elif g % 4 != 3 or g == 7:
                cg[0] = 0; cg[top] = top; xg[:, 0] = 15; xg[:, top] = 15; og[:, 0] = top * odd
                for t in range(RO):
                    v = D * (L - 1) + t; og[:, v] = top; xg[:, v] = 15
                    v = D * (L - 2) + t; og[:, v] = top * odd; xg[:, v] = 15
                    v = D + t; og[:, v] = top * (1 - odd); xg[:, v] = 15
                    xg[:, 2 * D + t] = 0
                    v = D * (L - 3) + t; z = D * (L - 1 - 2 * t) + D - 2; og[:, v] = top; xg[:, v] = 15
                    for k, a in ((14, z), (15, z - D)): og[k, v] = a; og[15, a] = v; xg[:, a] = 0; cg[a] = 0
    return pack(o, x, c)
def setup_inputs_corners(rng):
    o = meet(rng, 8, rng.integers(0, V, (N, 8, 8, V))); c = court(rng, 0.8, 1.0); x = rng.integers(0, 16, (N, 8, 16, V)); own = np.arange(V)
    kind = rng.integers(0, 8, (N, 8, 1, V)); x = np.where(kind == 0, 0, np.where(kind == 1, 15, x))
    for r in range(N):
        mo, ho = rng.permutation(8), rng.permutation(8)
        for g in range(8):
            og = o[r, g]; m, h = int(mo[g]), int(ho[g])
            if m == 0: c[r, g] = own
            elif m == 1: c[r, g] = 0
            elif m == 2: c[r, g] = V - 1
            elif m == 3: c[r, g] = (own + 1) % V
            elif m == 4: c[r, g] = V - 1 - own
            elif m == 5: c[r, g] = np.choose(rng.integers(0, 3, V), [np.zeros_like(own), own, np.full_like(own, V - 1)])
            if h in (0, 4): og[rng.integers(0, 16, V), own] = own
            elif h == 1: one = rng.random(V) < 0.3; og[:, one] = og[:1, one]
            elif h == 2: og[:] = np.choose(rng.integers(0, 3, (16, V)), [np.zeros((16, V), np.int64), np.broadcast_to(own, (16, V)), np.full((16, V), V - 1)])
            elif h == 3: og[3] = (own + 1) % V; og[12] = (own - 1) % V
    return pack(o, x, c)
def setup_inputs_ties(rng):
    o = meet(rng, 8, rng.integers(0, V, (N, 8, 8, V))); x = rng.integers(14, 16, (N, 8, 16, V)); c = np.zeros((N, 8, V), np.int64); idle = np.flatnonzero(np.arange(V) % D >= RO)
    for g in range(8):
        f = rng.permutation(idle)[:3]; f = f[:2 + g % 2]
        for r in range(N):
            c[r, g] = f[rng.integers(0, 2, V)]
            if g % 2: c[r, g] = np.where(rng.random(V) < 0.1, f[2], c[r, g])
            c[r, g, f] = f
            if g % 4 == 1: x[r, g] = 15
            elif g % 4 == 2:
                n = 9 if g == 2 else int(rng.integers(8, 11)); x[r, g] = (rng.permutation(16) < n).astype(np.int64)[:, None] * rng.integers(1, 16, (16, 1))
            elif g % 4 == 3: x[r, g] -= 7
    return pack(o, x, c)
def setup_inputs_rush(rng):
    o = meet(rng, 8, rng.integers(0, V, (N, 8, 8, V))); x = rng.integers(6, 16, (N, 8, 16, V)); low = rng.integers(0, 4, (N, 8, 16, V)); c = np.zeros((N, 8, V), np.int64)
    act, idle = np.flatnonzero(np.arange(V) % D < RO), np.flatnonzero(np.arange(V) % D >= RO)
    for g in range(8):
        f = rng.permutation(idle)[:2]; tp = {5: 0, 7: RO - 1}.get(g, -1)
        if tp >= 0: f[0] = D * int(rng.integers(0, L)) + tp
        for r in range(N):
            og = o[r, g]; k = rng.integers(0, 16, V); c[r, g] = np.where(rng.random(V) < 0.8, f[0], f[1]); z = act
            if g % 4 == 0: z = hubs(rng, og, L // 16)
            elif g % 4 == 1:
                for t in range(RO):
                    q = D * rng.permutation(L) + t; a, b = q[0::2], q[1::2]; og[k[a], a] = b; og[k[b], b] = a
            elif g % 4 == 2:
                og[k[act], act] = act; h = act[rng.random(len(act)) < 0.5]; og[(k[h] + 5) % 16, h] = h
            else:
                n = min(len(act), len(idle)); a, z = rng.permutation(act)[:n], rng.permutation(idle)[:n]
                for j in range(5): og[(k[a] + j) % 16, a] = z; og[(k[z] + j) % 16, z] = a
            c[r, g, z] = f[1]; x[r, g][:, z] = low[r, g][:, z]
            c[r, g, f] = f; x[r, g][:, f[0]] = 15
            if tp >= 0:
                h, y = [int(e) for e in rng.permutation(idle[idle != f[1]])[:2]]; i1, i2 = [int(e) for e in rng.permutation(16)[:2]]
                v = D * ((int(f[0]) // D + 1 + int(rng.integers(0, L - 1))) % L) + tp
                og[:, v] = h; og[i1, v] = f[0]; og[i2, v] = y; og[int(rng.integers(0, 16)), y] = v
                og[:, f[0]] = h; og[int(rng.integers(0, 16)), f[0]] = v
                c[r, g, h] = f[0]; c[r, g, v] = f[1]; c[r, g, y] = f[1]; x[r, g][:, h] = 15; x[r, g][:, v] = rng.integers(1, 4, 16)
    return pack(o, x, c)
def check_inputs(d):
    bad = []
    for k, hi in (("hol", V - 1), ("sha", 15), ("ctl", V - 1)):
        v = np.asarray(d[k]).astype(np.float64)
        if not (np.min(v) >= 0 and np.max(v) <= hi): bad.append("range of " + k)
        elif np.any(v != np.floor(v)): bad.append("whole numbers of " + k)
    return bad
def reference(hol, sha, ctl):
    o = hol.astype(np.int64).reshape(N, 8, 16, V); x = sha.astype(np.float32).astype(np.int64).reshape(N, 8, 16, V); c = ctl.astype(np.int64)
    last = np.zeros(N, np.int64)
    for t in range(RO):
        d = 1 + t % (N - 1); vs = D * np.arange(L) + t
        no, nc, wins = [], [], []
        for r in range(N):
            a = o[r][:, :, vs]; af = a.reshape(8, 16 * L); cf = af
            for h in range(HOP): cf = np.take_along_axis(c[(r + h * d) % N], cf, 1)
            ck = cf.reshape(8, 16, L)
            xk = np.take_along_axis(x[r], af[:, None, :], 2).reshape(8, 16, 16, L); xv = x[r][:, :, vs]
            m = np.add.reduce(np.minimum(xk, xv[:, :, None, :]), axis=1)
            pool = np.add.reduce(np.where(ck[:, :, None, :] == ck[:, None, :, :], m[:, None, :, :], 0), axis=2)
            kb = np.argmax(pool, axis=1)
            b = np.take_along_axis(ck, kb[:, None, :], 1)[:, 0]
            mine = ck == b[:, None, :]
            part = np.add.reduce(np.where(mine[:, None, :, :], xk, 0), axis=2); full = np.add.reduce(xk, axis=2)
            win = np.add.reduce((2 * part > full).astype(np.int64), axis=1) >= 9 + (last[r] & 1)
            ok = np.take_along_axis(o[r], af[:, None, :], 2).reshape(8, 16, 16, L)
            stake = np.any(ok == vs, axis=1)
            xb = np.take_along_axis(x[r], b[:, None, :], 2)
            far = np.where(stake & ~mine, np.add.reduce(np.abs(xk - xb[:, :, None, :]), axis=1), -1)
            ks = np.argmax(far, axis=1); sells = win & (np.max(far, axis=1) >= 0)
            goal = np.take_along_axis(a, ks[:, None, :], 1)[:, 0]; cs = np.take_along_axis(ck, ks[:, None, :], 1)[:, 0]
            on = o[r] + 0; cn = c[r] + 0
            for g in range(8):
                ln = np.flatnonzero(sells[g]); tg, first = np.unique(goal[g, ln], return_index=True); w = ln[first]
                col = o[r, g][:, tg]; on[g][:, tg] = np.where(col == vs[w], cs[g, w], col)
                on[g, ks[g, ln], vs[ln]] = b[g, ln]
            cn[:, vs] = np.where(win, b, vs)
            no.append(on); nc.append(cn); wins.append(np.add.reduce(win.astype(np.int64).reshape(-1)))
        o = np.stack(no); c = np.stack(nc); last = np.array(wins, np.int64)
    return {"yo": o.reshape(N, 128, V).astype(np.float32), "yc": c.astype(np.float32)}

@@ -1,0 +1,582 @@
+from concourse.bass import DstId, RemoteDMATransfer
+from concourse.mybir import dt, AluOpType, AxisListType, ActivationFunctionType
+
+V_, RO, NR = 3072, 4, 4
+PAD = 256
+OP = AluOpType
+COPY = ActivationFunctionType.Copy
+IDENT = ActivationFunctionType.Identity
+
+
+def _decl():
+    s = {}
+
+    def sb(name, shape, dtype):
+        s[name] = ("sbuf", shape, dtype)
+    f, b, i, u = "float32", "bfloat16", "int32", "uint16"
+    sb("O", [128, V_ + PAD], f); sb("OI", [128, V_], i); sb("XX", [128, 2 * V_], b); sb("CC", [128, V_], b)
+    for d in (1, 2, 3): sb("WC%d" % d, [128, V_], b)
+    sb("CI", [128, 192], i); sb("CF", [128, 192], f); sb("HL0", [128, 384], b)
+    sb("TI", [128, 192], i); sb("TF", [128, 192], f); sb("CLf", [128, 192], f); sb("CLk", [128, 192], f); sb("CLu", [128, 192], u)
+    for r in range(NR): sb("L0_%d" % r, [128, 384], b)
+    sb("LU", [128, 12, 2, 8, 2], b); sb("SND", [128, 3, 2, 8, 2], b)
+    for t in range(2): sb("VT%d" % t, [128, 4096], f)
+    sb("VR", [128, 4, 256], f); sb("PM", [128, 4, 128], f); sb("KP", [128, 4, 96], f)
+    sb("VC", [128, 16], f)
+    for n in ("XK", "CG", "ST", "MN", "XM"): sb(n, [128, 2, 2048], b)
+    sb("MX", [128, 2, 4, 8, 64], b); sb("E", [128, 2, 8, 8, 16], b); sb("PR", [128, 2, 15, 8, 16], b)
+    for n in ("cS", "RM", "BR", "oh", "w", "brep", "LMf", "BD", "cKv", "q2", "pz", "pc", "nC0", "nC", "BDc", "OC", "OE"): sb(n, [128, 2, 128], f)
+    for n in ("nm", "XB", "wp", "win", "ew", "oh2_"): sb(n, [128, 2, 128], b)
+    sb("mS", [128, 2, 8, 24], b); sb("LM", [128, 256], u); sb("BZ", [128, 2, 128], f); sb("kS", [128, 2, 128], f); sb("HLz", [128, 2, 8, 16], b)
+    sb("LA", [128, 256], u); sb("LB", [128, 16], u); sb("ZL", [128, 16], u); sb("FZ", [128, 16], u); sb("ZU", [128, 256], u)
+    for n in ("aD", "oK", "ZQ", "ZS", "NC", "nlq", "fz", "FS", "XO", "DM", "QM"): sb(n, [128, 256], f)
+    sb("fl", [128, 16], f); sb("DL", [128, 16], f); sb("DE", [128, 4096], b)
+    for n in ("Ib", "Im", "I256", "I16", "I3072", "BOb", "L4", "LW", "ONE", "K1", "K2"): sb(n, [128, 128], b)
+    for n in ("If", "BOf", "NF"): sb(n, [128, 128], f)
+    for n in ("DC", "DR"): sb(n, [128, 256], b)
+    for n in ("S1", "S16", "S32", "Sm16", "SHL"): sb(n, [128, 8], b)
+    sb("U8", [128, 8], f); sb("U4", [128, 96], f)
+    sb("ci", [128, 256], f); sb("cg", [128, 256], f); sb("cq", [128, 256], f)
+    sb("pi", [128, 1], i); sb("ti", [128, 16], i); sb("tf", [128, 16], f); sb("wq", [128, 16], f)
+    sb("zr", [128, 4], f); sb("zi", [128, 4], i); sb("Zc", [128, 1], f)
+    for n in ("pA0", "pA1", "pB0", "pB1", "pC0", "pC1", "pD"): s[n] = ("psum", [128, 8, 64], f)
+    s["pE"] = ("psum", [128, 512], f)
+    return s
+
+
+SCRATCH = _decl()
+SEMAPHORES = ["cV", "cS", "cP", "cG", "loc"] + ["d%d" % k for k in range(52)] + ["ar%d_%d" % (t, r) for t in range(4) for r in range(NR)]
+PS = ("pA0", "pA1", "pB0", "pB1", "pC0", "pC1", "pD", "pE")
+D_OF = [1 + t % 3 for t in range(RO)]
+CYC = 0.83e-3
+WAKE = 0.09
+GCY = 1.5
+ASG = {"XK0": "S", "XK1": "S", "CG0": "S", "CG1": "S", "XM0": "S", "XM1": "S"}
+MXS = ()
+PRS = ()
+
+
+def new_graph():
+    return {"ops": [], "wr": {}, "rd": {}, "bw": {}, "br": {}}
+
+
+def add(G, opts, fn, r=(), w=(), pr=(), pw=(), key=None, cnt=1, name=""):
+    n = len(G["ops"])
+    deps = {}
+
+    def dep(j, raw):
+        if j != n: deps[j] = deps.get(j, False) or raw
+    for (bn, lo, hi) in r:
+        for (a, b, j) in G["wr"].get(bn, []):
+            if a < hi and lo < b: dep(j, True)
+        G["rd"].setdefault(bn, []).append((lo, hi, n))
+    for (bn, lo, hi) in w:
+        for (a, b, j) in G["wr"].get(bn, []):
+            if a < hi and lo < b: dep(j, False)
+        for (a, b, j) in G["rd"].get(bn, []):
+            if a < hi and lo < b: dep(j, False)
+        G["wr"][bn] = [x for x in G["wr"].get(bn, []) if not (lo <= x[0] and x[1] <= hi)] + [(lo, hi, n)]
+        G["rd"][bn] = [x for x in G["rd"].get(bn, []) if not (lo <= x[0] and x[1] <= hi)]
+    engs = tuple(sorted(opts))
+    for bn in pr:
+        if bn in G["bw"]: dep(G["bw"][bn], True)
+        for j in G["br"].get(bn, []):
+            if G["ops"][j]["engs"] != engs or len(engs) > 1: dep(j, False)
+        G["br"].setdefault(bn, []).append(n)
+    for bn in pw:
+        if bn in G["bw"]: dep(G["bw"][bn], False)
+        for j in G["br"].get(bn, []): dep(j, False)
+        G["bw"][bn] = n; G["br"][bn] = []
+    G["ops"].append({"opts": opts, "engs": engs, "fn": fn, "deps": deps, "key": key, "cnt": cnt, "name": name})
+    return n
+
+
+def schedule(G, wake=WAKE, quant=0.12):
+    ops = G["ops"]; n = len(ops)
+    succ = [[] for _ in range(n)]; ind = [len(o["deps"]) for o in ops]
+    for i, o in enumerate(ops):
+        for j in o["deps"]: succ[j].append(i)
+    prio = [0.0] * n
+    for i in range(n - 1, -1, -1):
+        d = min(x[1] for x in ops[i]["opts"].values())
+        prio[i] = d + max([prio[s] + 0.5 * wake for s in succ[i]] or [0.0])
+    free = {}; fin = [0.0] * n; eng = [None] * n; rdy = {}
+    order = []; t_ready = [0.0] * n
+    for i in range(n):
+        if ind[i] == 0: rdy[i] = True
+    while rdy:
+        best = None
+        for i in rdy:
+            for e, c in ops[i]["opts"].items():
+                st = free.get(e, 0.0)
+                for j, raw in ops[i]["deps"].items():
+                    x = fin[j] + (wake if eng[j] != e else (0.06 if raw else -1.0))
+                    if x > st: st = x
+                k = (int(st / quant), -prio[i], st)
+                if best is None or k < best[0]: best = (k, i, e, st)
+        _, i, e, st = best
+        del rdy[i]
+        c = ops[i]["opts"][e]
+        free[e] = st + c[0]; fin[i] = st + c[1]; eng[i] = e; t_ready[i] = st
+        order.append(i)
+        for s in succ[i]:
+            ind[s] -= 1
+            if ind[s] == 0: rdy[s] = True
+    return order, eng, fin, t_ready
+
+
+def vc(n, two=1.0): return max(64.0, n * two) * CYC * 1.2 + 0.01
+def sc(n): return max(64.0, n) * CYC * 1.2 + 0.03
+def pc_(n, f32=False): return max(64.0, n) * CYC * (4.0 if f32 else 1.0) + 0.01
+
+
+def build(core, T, topo, rank):
+    G = new_graph()
+    W = lambda n: (n, 0, 1 << 20)
+    nd = [0]
+
+    def vop(fn, n, r=(), w=(), pr=(), pw=(), two=1.0, name=""):
+        c = vc(n, two)
+        return add(G, {"V": (c, c)}, lambda Q, e: fn(Q["V"]), r, w, pr, pw, name=name)
+
+    def tt(o, a, b, op, n, r=(), w=(), pr=(), name="", pw=(), two=None):
+        vop(lambda v: v.tensor_tensor(o, a, b, op), n, r, w, pr, pw, two=two or (1.0 if pr else 2.0), name=name)
+
+    def ts(o, a, s1, op0, n, r=(), w=(), pr=(), s2=None, op1=None, two=1.0, name=""):
+        if op1 is None: vop(lambda v: v.tensor_scalar(o, a, s1, None, op0), n, r, w, pr, two=two, name=name)
+        else: vop(lambda v: v.tensor_scalar(o, a, s1, s2, op0, op1), n, r, w, pr, two=two, name=name)
+
+    def cpv(o, a, n, r=(), w=(), pr=(), name=""):
+        vop(lambda v: v.tensor_copy(o, a), n, r, w, pr, name=name)
+
+    def flex(o, a, n, r=(), w=(), pr=(), name="", cyc=1.0, only=None):
+        opts = {"V": (vc(n, cyc), vc(n, cyc)), "S": (sc(n * cyc), sc(n * cyc))}
+        only = only or ASG.get(name)
+        if only: opts = {only: opts[only]}
+        return add(G, opts, lambda Q, e: Q["V"].tensor_copy(o, a) if e == "V" else Q["S"].activation(o, a, COPY), r, w, pr, name=name)
+
+    def act(o, a, n, func=COPY, bias=0.0, scale=1.0, r=(), w=(), pr=(), name="", pw=()):
+        return add(G, {"S": (sc(n), sc(n))}, lambda Q, e: Q["S"].activation(o, a, func, bias=bias, scale=scale), r, w, pr, pw, name=name)
+
+    def mm(o, l, rh, start, stop, bank, n, r=(), f32=False, name=""):
+        c = pc_(n, f32)
+        return add(G, {"P": (c, c)}, lambda Q, e: Q["P"].matmul(o, l, rh, start, stop), r, (), (), (bank,), name=name)
+
+    def gop(fn, n, r=(), w=(), name=""):
+        c = 0.14 + 2 * n * CYC * 1.2
+        return add(G, {"G": (c, c)}, lambda Q, e: fn(Q["G"]), r, w, name=name)
+
+    def dma(o, a, kb, r=(), w=(), q="Y", name=""):
+        k = nd[0]; nd[0] += 1
+        return add(G, {q: (0.1, 2.0 + kb / 200.0)}, lambda Q, e: (Q["Y"] if e == "Y" else Q["S"]).dma_start(o, a).then_inc(T.sem["d%d" % k], 16), r, w, key="d%d" % k, cnt=16, name=name)
+
+    def send(dsts, src_ap, land, sem, r, kb, name):
+        m = 255
+        ne = len(topo.engines(core, dsts[0]))
+        for x in dsts: assert topo.may_write(core, x) and topo.mask(core, x) == topo.mask(core, dsts[0])
+
+        def fn(Q, e):
+            if len(dsts) == 1:
+                rid, pid = topo.addr(dsts[0])[:2]
+                Q["G"].remote_dma(out_ap=land, in_ap=src_ap, remote_sem=T.sem[sem], local_sem=T.sem.loc, pid=pid, routing_id=rid, dma_engine_mask=topo.mask(core, dsts[0]))
+            else:
+                ids = [DstId(rid=topo.addr(x)[0], pnc=topo.addr(x)[1]) for x in dsts]
+                Q["G"].remote_dma_fused([RemoteDMATransfer(dst_ids=ids, dma_engine_mask=topo.mask(core, dsts[0]), remote_sem=T.sem[sem], srcs=[src_ap], dsts=[land for x in dsts])], local_sem=T.sem.loc)
+        return add(G, {"G": (1.0, 1.0)}, fn, r, (), key="loc", cnt=ne, name=name)
+
+    def arrive(src_rank, t, after, kb):
+        nm = "L%d_%d" % (t, src_rank)
+        i = add(G, {"N%d_%d" % (t, src_rank): (0.0, 2.5 + kb / 40.0)}, None, (), (W(nm),), key="ar%d_%d" % (t, src_rank), cnt=len(topo.engines(T.cores[src_rank], core)), name="arrive")
+        G["ops"][i]["deps"][after] = True
+
+    H = (0, 1)
+
+    def ext(X, bank):
+        add(G, {"S": (sc(64), sc(64))}, lambda Q, e: Q["S"].activation(X[:, :, 16:24], X[:, :, 0:8], COPY), (), (), (bank,), (bank,), name="ext")
+
+    def P(n, h): return T["p" + n + str(h)]
+    def B(n, h): return T[n][:, h]
+    def LU(t, r): return T.LU[:, 4 * (t - 1) + r]
+
+    dma(T.CI[:], T.ctl[:], 98, w=[W("CI")], name="ld ctl")
+    for c in range(4):
+        dma(T.OI[:, 768 * c:768 * c + 768], T.hol[:, 768 * c:768 * c + 768], 393, w=[("OI", 768 * c, 768 * c + 768)], q="Y", name="ld hol")
+    for e in range(2):
+        for b in range(6):
+            dma(T.TI[:, 32 * b + 16 * e:32 * b + 16 * e + 16], T.ctl[e::2, 512 * b:512 * b + 512], 8, w=[("TI", 32 * b + 16 * e, 32 * b + 16 * e + 16)], q="S", name="ld list")
+    for c in range(2):
+        dma(T.XX[:, 1536 * c:1536 * c + 1536], T.sha[:, 1536 * c:1536 * c + 1536], 393, w=[("XX", 1536 * c, 1536 * c + 1536)], q="S", name="ld sha")
+    cpv(T.CF[:], T.CI[:], 192, r=[W("CI")], w=[W("CF")], name="CF")
+    cpv(T.HL0[:, 0:192], T.CF[:], 192, r=[W("CF")], w=[("HL0", 0, 192)])
+    tt(T.HL0[:, 192:384], T.CF[:], T.HL0[:, 0:192], OP.subtract, 192, r=[W("CF"), ("HL0", 0, 192)], w=[("HL0", 192, 384)])
+    me = T.cores[rank]
+    first = T.cores[(rank - D_OF[0]) % NR]
+    rest = [T.cores[(rank - d) % NR] for d in (1, 2, 3) if (rank - d) % NR != (rank - D_OF[0]) % NR]
+    lands = "L0_%d" % rank
+    s1 = send([first], T.HL0[:], T[lands][:], "ar0_%d" % rank, [W("HL0")], 98, "send0")
+    s2 = send(rest, T.HL0[:], T[lands][:], "ar0_%d" % rank, [W("HL0")], 196, "send0b")
+    gop(lambda g: g.iota(T.pi[:], [[1, 1]], 0, 1), 1, w=[W("pi")])
+    gop(lambda g: g.iota(T.ci[:], [[1, 256]], 0, 0, allow_small_or_imprecise_dtypes=True), 256, w=[W("ci")])
+    gop(lambda g: g.iota(T.cg[:], [[1, 16], [0, 16]], 0, 0, allow_small_or_imprecise_dtypes=True), 256, w=[W("cg")])
+    gop(lambda g: g.iota(T.cq[:], [[0, 16], [1, 16]], 0, 0, allow_small_or_imprecise_dtypes=True), 256, w=[W("cq")])
+    gop(lambda g: g.iota(T.DL[:], [[16, 16]], V_, 0, allow_small_or_imprecise_dtypes=True), 16, w=[W("DL")])
+    gop(lambda g: g.iota(T.DM[:], [[1, 256]], V_, 0, allow_small_or_imprecise_dtypes=True), 256, w=[W("DM")])
+    for t in range(RO):
+        gop(lambda g, t=t: g.iota(T.VR[:, t], [[12, 256]], t, 0, allow_small_or_imprecise_dtypes=True), 256, w=[W("VR%d" % t)])
+
+    def vt(t):
+        for c in range(4):
+            i = gop(lambda g, c=c: g.iota(T["VT%d" % (t % 2)][:, 1024 * c:1024 * c + 1024], [[12, 64], [0, 16]], t + 768 * c, 0, allow_small_or_imprecise_dtypes=True), 1024, w=[("VT%d" % (t % 2), 1024 * c, 1024 * c + 1024)], name="VT")
+            G["ops"][i]["deps"][s2] = False
+    vt(0)
+    vt(1)
+    for d in (1, 2, 3): vop(lambda v, d=d: v.memset(T["WC%d" % d][:], 0.0), V_, w=[W("WC%d" % d)], two=0.5)
+    for d in (1, 2, 3):
+        s = (rank + d) % NR
+        arrive(s, 0, s1 if d == D_OF[0] else s2, 98 if d == D_OF[0] else 196)
+        for x in (0, 1):
+            dma(T["WC%d" % d][x:128:16, :], T["L0_%d" % s][:, 192 * x:192 * x + 192], 49, r=[W("L0_%d" % s)], w=[W("WC%d" % d)] if x == 0 else [("WC%d" % d, 0, 1 << 19)], name="flat")
+            if x == 0: G["wr"]["WC%d" % d] = [y for y in G["wr"]["WC%d" % d]]
+    def sh(o, k): ts(T.ti[:, o:o + 1], T.pi[:], k, OP.arith_shift_right, 1, r=[W("pi")], w=[("ti", o, o + 1)])
+    def an(o, src, k, rr): ts(T.ti[:, o:o + 1], src, k, OP.bitwise_and, 1, r=rr, w=[("ti", o, o + 1)])
+    sh(1, 4); an(2, T.pi[:], 15, [W("pi")])
+    cpv(T.ti[:, 0:1], T.pi[:], 1, r=[W("pi")], w=[("ti", 0, 1)])
+    an(8, T.pi[:], 3, [W("pi")])
+    ts(T.ti[:, 9:10], T.ti[:, 8:9], 12, OP.mult, 1, r=[("ti", 8, 9)], w=[("ti", 9, 10)])
+    for t in range(RO):
+        ts(T.ti[:, 10 + t:11 + t], T.ti[:, 9:10], t, OP.add, 1, r=[("ti", 9, 10)], w=[("ti", 10 + t, 11 + t)])
+        an(3 + t, T.ti[:, 10 + t:11 + t], 15, [("ti", 10 + t, 11 + t)])
+    ts(T.ti[:, 14:15], T.pi[:], 12, OP.mult, 1, r=[W("pi")], w=[("ti", 14, 15)])
+    ts(T.ti[:, 7:8], T.ti[:, 14:15], 4, OP.arith_shift_right, 1, r=[("ti", 14, 15)], w=[("ti", 7, 8)])
+    ts(T.ti[:, 15:16], T.ti[:, 1:2], 8, OP.add, 1, r=[("ti", 1, 2)], w=[("ti", 15, 16)])
+    cpv(T.tf[:], T.ti[:], 16, r=[W("ti")], w=[W("tf")])
+    F = lambda k: T.tf[:, k:k + 1]
+    tfr = [W("tf")]
+    for h in H:
+        for t in range(RO):
+            k = 2 * t + h
+            ts(T.VC[:, k:k + 1], F(0), 12.0, OP.mult, 1, r=tfr, w=[("VC", k, k + 1)], s2=float(12 * 128 * h + t), op1=OP.add)
+            ts(T.VC[:, 8 + k:9 + k], F(0), -12.0, OP.mult, 1, r=tfr, w=[("VC", 8 + k, 9 + k)], s2=float(-12 * 128 * h - t), op1=OP.add)
+    ts(T.DL[:], T.DL[:], F(2), OP.add, 16, r=tfr + [W("DL")], w=[W("DL")])
+    ci = T.ci[:, 0:128]; rc = tfr + [W("ci")]; rq = tfr + [W("cq")]; rg = tfr + [W("cg")]
+    ts(T.If[:], ci, F(0), OP.is_equal, 128, r=rc, w=[W("If")])
+    for nmx, s in (("Ib", 1.0), ("Im", -1.0), ("I256", -256.0), ("I16", 16.0), ("I3072", 3072.0)):
+        ts(T[nmx][:], ci, F(0), OP.is_equal, 128, r=rc, w=[W(nmx)], s2=s, op1=OP.mult)
+    ts(T.BOf[:], T.cg[:, 0:128], F(1), OP.is_equal, 128, r=rg, w=[W("BOf")])
+    for nmx, s in (("BOb", 1.0), ("L4", 4.0)):
+        ts(T[nmx][:], T.cg[:, 0:128], F(1), OP.is_equal, 128, r=rg, w=[W(nmx)], s2=s, op1=OP.mult)
+    ts(T.QM[:], T.cq[:], F(2), OP.is_equal, 256, r=rq, w=[W("QM")])
+    ts(T.NF[:], T.cq[:, 0:128], 0.0, OP.not_equal, 128, r=[W("cq")], w=[W("NF")])
+    for nmx, s in (("S1", 1.0), ("S16", 16.0), ("S32", 32.0), ("Sm16", -16.0)):
+        ts(T[nmx][:], T.ci[:, 0:8], F(1), OP.is_equal, 8, r=rc, w=[W(nmx)], s2=s, op1=OP.mult)
+    ts(T.wq[:, 0:1], F(2), 1.0, OP.is_le, 1, r=tfr, w=[("wq", 0, 1)])
+    ts(T.SHL[:], T.ci[:, 0:8], F(1), OP.is_equal, 8, r=rc + [("wq", 0, 1)], w=[W("SHL")], s2=T.wq[:, 0:1], op1=OP.mult)
+    ts(T.U8[:], T.ci[:, 0:8], F(1), OP.is_equal, 8, r=rc, w=[W("U8")])
+    ts(T.U4[:], T.ci[:, 0:96], F(7), OP.is_equal, 96, r=rc, w=[W("U4")])
+    for t in range(RO): ts(T.PM[:, t], T.cq[:, 0:128], F(3 + t), OP.is_equal, 128, r=rq, w=[W("PM%d" % t)])
+    ts(T.K1[:], T.cq[:, 0:128], -1.0, OP.mult, 128, r=[W("cq")], w=[W("K1")], s2=15.0, op1=OP.add)
+    ts(T.K2[:], T.cq[:, 0:128], -1.0, OP.mult, 128, r=[W("cq")], w=[W("K2")], s2=31.0, op1=OP.add)
+    vop(lambda v: v.memset(T.ONE[:], 1.0), 128, w=[W("ONE")])
+    for q in range(16): vop(lambda v, q=q: v.memset(T.fz[:, q::16], 2.0 ** -q), 16, w=[W("fz")])
+    tt(T.FS[:], T.fz[:], T.QM[:], OP.mult, 256, r=[W("fz"), W("QM")], w=[W("FS")])
+    vop(lambda v: v.tensor_reduce(T.wq[:, 1:2], T.FS[:, 0:16], AxisListType.X, OP.add), 16, r=[W("FS")], w=[("wq", 1, 2)])
+    ts(T.LW[:], T.BOf[:], T.wq[:, 1:2], OP.mult, 128, r=[W("BOf"), ("wq", 1, 2)], w=[W("LW")])
+    ts(T.nlq[:], T.QM[:], 64.0, OP.mult, 256, r=[W("QM")], w=[W("nlq")], s2=-64.0, op1=OP.add)
+    ts(T.ZQ[:], T.FS[:], -2.0, OP.mult, 256, r=[W("FS")], w=[W("ZQ")])
+    tt(T.DC[:], T.nlq[:], T.ZQ[:], OP.add, 256, r=[W("nlq"), W("ZQ")], w=[W("DC")])
+    ts(T.wq[:, 2:3], F(0), 0.0, OP.is_equal, 1, r=tfr, w=[("wq", 2, 3)], s2=float(V_), op1=OP.mult)
+    ts(T.wq[:, 3:4], F(0), 1.0, OP.is_equal, 1, r=tfr, w=[("wq", 3, 4)])
+    ts(T.DR[:], T.ci[:], T.wq[:, 3:4], OP.mult, 256, r=[W("ci"), ("wq", 2, 4)], w=[W("DR")], s2=T.wq[:, 2:3], op1=OP.add)
+    vop(lambda v: v.memset(T.O[:, V_:V_ + PAD], 0.0), PAD, w=[("O", V_, V_ + PAD)])
+    for h in H:
+        vop(lambda v, h=h: v.memset(B("BZ", h)[:], 0.0), 128, w=[W("BZ%d" % h)])
+        vop(lambda v, h=h: v.memset(B("HLz", h)[:], 0.0), 128, w=[W("HLz%d" % h)])
+    vop(lambda v: v.memset(T.Zc[:], 9.0), 1, w=[W("Zc")])
+    for t in range(RO):
+        mm(T.pE[:, 0:96], T.PM[:, t], T.U4[:], True, True, "pE", 96, r=[W("PM%d" % t), W("U4")], f32=True)
+        ts(T.KP[:, t], T.pE[:, 0:96], -1.0, OP.mult, 96, w=[W("KP%d" % t)], pr=["pE"], s2=1.0, op1=OP.add)
+    cpv(T.TF[:], T.TI[:], 192, r=[W("TI")], w=[W("TF")])
+    vop(lambda v: v.transpose(T.CLf[:], T.TF[:]), 192, r=[W("TF")], w=[W("CLf")])
+    cpv(T.CLu[:], T.CLf[:], 192, r=[W("CLf")], w=[W("CLu")])
+    for c in range(4):
+        cpv(T.O[:, 768 * c:768 * c + 768], T.OI[:, 768 * c:768 * c + 768], 768, r=[("OI", 768 * c, 768 * c + 768)], w=[("O", 768 * c, 768 * c + 768)], name="O f32")
+    for c in range(2):
+        a, z = 1536 * c, 1536 * c + 1536
+        add(G, {"V": (vc(1536, 0.5), vc(1536, 0.5)), "S": (sc(1536), sc(1536))},
+            lambda Q, e, a=a, z=z: Q["V"].tensor_scalar(T.XX[:, V_ + a:V_ + z], T.XX[:, a:z], -1.0, None, OP.mult) if e == "V" else Q["S"].activation(T.XX[:, V_ + a:V_ + z], T.XX[:, a:z], COPY, scale=-1.0),
+            [("XX", a, z)], [("XX", V_ + a, V_ + z)], name="-X")
+
+    for t in range(RO):
+        d = D_OF[t]; last = t == RO - 1
+        wc = "WC%d" % d
+        VT, VR = T["VT%d" % (t % 2)], T.VR[:, t]
+        XR = [("XX", 0, V_)]
+        hs = lambda h: slice(1536 * h + t, 1536 * h + 1536, 12)
+        oreg = lambda h: ("O", 1536 * h, 1536 * h + 1536)
+        S = lambda h: slice(128 * h, 128 * h + 128)
+        for h in H:
+            src = T.OI if t == 0 else T.O
+            cpv(T.LA[:, S(h)], src[:, hs(h)], 128, r=[("OI" if t == 0 else "O", 1536 * h, 1536 * h + 1536)], w=[("LA", 128 * h, 128 * h + 128)], name="LA")
+        for c in range(4):
+            flex(T.CC[:, 768 * c:768 * c + 768], T[wc][:].indirect(T.CLu[:, 48 * c:48 * c + 48]), 768, r=[W(wc), W("CLu")], w=[("CC", 768 * c, 768 * c + 768)], cyc=GCY, name="compose%d" % c)
+        la = lambda h: ("LA", 128 * h, 128 * h + 128)
+        for h in H: flex(B("XK", h)[:], T.XX[:, 0:V_].indirect(T.LA[:, S(h)]), 2048, r=XR + [la(h)], w=[W("XK%d" % h)], cyc=GCY, name="XK%d" % h)
+        for h in H: flex(B("CG", h)[:], T.CC[:].indirect(T.LA[:, S(h)]), 2048, r=[W("CC"), la(h)], w=[W("CG%d" % h)], cyc=GCY, name="CG%d" % h)
+        for h in H:
+            vop(lambda v, h=h, VT=VT: v.tensor_tensor(B("ST", h)[:], T.O[:, 0:V_].indirect(T.LA[:, S(h)]), VT[:, 2048 * h:2048 * h + 2048], OP.is_equal), 2048,
+                r=[("O", 0, V_), la(h), ("VT%d" % (t % 2), 2048 * h, 2048 * h + 2048)], w=[W("ST%d" % h)], two=GCY, name="ST")
+        if t + 2 < RO: vt(t + 2)
+        for h in H:
+            mm(P("C", h)[:, :, 0:16], T.Ib[:], T.XX[:, hs(h)], True, True, "pC%d" % h, 128, r=XR + [W("Ib")])
+        for h in H:
+            A = P("A", h); bk = "pA%d" % h
+            for k in range(16):
+                mm(A[:, :, k], B("CG", h)[:, k::16], T.SHL[:], True, True, bk, 8, r=[W("CG%d" % h), W("SHL")], name="cL")
+            ext(A, bk)
+            flex(B("cS", h)[:], A[:, :, 0:16], 128, w=[W("cS%d" % h)], pr=[bk], name="cS")
+            for s in range(1, 9):
+                tt(B("E", h)[:, s - 1], B("cS", h)[:], A[:, :, s:s + 16], OP.not_equal if h in PRS else OP.is_equal, 128, r=[W("cS%d" % h)], w=[("E%d" % h, s - 1, s)], pr=[bk], name="E")
+        for h in H:
+            Bk = P("B", h); bk = "pB%d" % h
+            for k in range(16):
+                tt(B("MN", h)[:, S(k)], B("XK", h)[:, k::16], P("C", h)[:, :, 0:16], OP.min, 128, r=[W("XK%d" % h)], w=[("MN%d" % h, 128 * k, 128 * k + 128)], pr=["pC%d" % h], name="MN")
+            for k in range(16):
+                mm(Bk[:, :, k], B("MN", h)[:, S(k)], T.S1[:], True, True, bk, 8, r=[("MN%d" % h, 128 * k, 128 * k + 128), W("S1")], name="mL")
+            ext(Bk, bk)
+            mS = B("mS", h)
+            flex(mS[:], Bk[:, :, 0:24], 192, w=[W("mS%d" % h)], pr=[bk], name="mS", only="S")
+            PRh, Eh = B("PR", h), B("E", h)
+            for c in range(4 if h in PRS else 0):
+                bn = "pE" if c % 2 else bk
+                n = min(4, 15 - 4 * c)
+                for jj in range(n):
+                    j = 4 * c + jj
+                    s = j + 1 if j < 8 else j - 7
+                    o = T.pE[:, S(jj)] if c % 2 else Bk[:, 2 * jj:2 * jj + 2, :]
+                    mm(o, T.Ib[:], mS[:, :, s:s + 16] if j < 8 else mS[:, :, 0:16], True, False, bn, 128, r=[W("mS%d" % h), W("Ib")], name="PRm")
+                    mm(o, T.I256[:], Eh[:, s - 1], False, True, bn, 128, r=[("E%d" % h, s - 1, s), W("I256")], name="PRm")
+                act(PRh[:, 4 * c:4 * c + n], T.pE[:, 0:128 * n] if c % 2 else Bk[:, 0:2 * n, :], 128 * n, ActivationFunctionType.Relu, w=[("PR%d" % h, 4 * c, 4 * c + n)], pr=[bn], name="PRa")
+            for s in range(1, 9 if h not in PRS else 0):
+                tt(PRh[:, s - 1], Eh[:, s - 1], Bk[:, :, s:s + 16], OP.mult, 128, r=[("E%d" % h, s - 1, s)], w=[("PR%d" % h, s - 1, s)], pr=[bk], name="PR")
+            for s in range(1, 8 if h not in PRS else 0):
+                tt(PRh[:, 7 + s], Eh[:, s - 1], Bk[:, :, 0:16], OP.mult, 128, r=[("E%d" % h, s - 1, s)], w=[("PR%d" % h, 7 + s, 8 + s)], pr=[bk], name="PR")
+            C = P("C", h); ck = "pC%d" % h
+            mm(C[:, :, 16:32], T.Ib[:], T.K1[:], True, False, ck, 128, r=[W("Ib"), W("K1")], name="key")
+            mm(C[:, :, 16:32], T.I16[:], mS[:, :, 0:16], False, False, ck, 128, r=[W("I16"), W("mS%d" % h)], name="key")
+            for s in range(1, 9):
+                mm(C[:, :, 16:32], T.I16[:], PRh[:, s - 1], False, False, ck, 128, r=[("PR%d" % h, s - 1, s)], name="key")
+            for s in range(1, 8):
+                mm(C[:, :, 16 + s:32], T.I16[:], PRh[:, 7 + s, :, 0:16 - s], False, False, ck, 128 - 8 * s, r=[("PR%d" % h, 7 + s, 8 + s)], name="key")
+                mm(C[:, :, 16:16 + s], T.I16[:], PRh[:, 7 + s, :, 16 - s:16], False, s == 7, ck, 8 * s, r=[("PR%d" % h, 7 + s, 8 + s)], name="key")
+
+        def spread(h, src, sreg, fin, freg, floor=None, bank=None):
+            bz = B("BZ", h); zr = [W("BZ%d" % h)]
+            if floor is None: cpv(bz[:, 0::16], src[:, 15::16], 8, r=[sreg], w=zr, name="sp")
+            else: ts(bz[:, 0::16], src[:, 15::16], floor, OP.max, 8, r=[sreg], w=zr, name="sp")
+            vop(lambda v: v.tensor_tensor_scan(fin, T.NF[:], bz[:], 0.0, OP.mult, OP.add), 128, r=zr + [W("NF")], w=[freg] if freg else [], pw=[bank] if bank else [], name="sp")
+
+        for h in H:
+            A, C = P("A", h), P("C", h); ak, ck = "pA%d" % h, "pC%d" % h
+            x = lambda n: W(n + str(h))
+            act(B("kS", h)[:], C[:, :, 16:32], 128, w=[x("kS")], pr=[ck], name="kS")
+            vop(lambda v, h=h: v.tensor_tensor_scan(B("RM", h)[:], T.NF[:], B("kS", h)[:], 0.0, OP.mult, OP.max), 128, r=[W("NF"), x("kS")], w=[x("RM")], name="RM")
+            spread(h, B("RM", h), x("RM"), B("BR", h), x("BR"))
+            tt(B("oh", h)[:], B("BR", h)[:], C[:, :, 16:32], OP.is_equal, 128, r=[x("BR")], w=[x("oh")], pr=[ck], name="oh")
+            tt(B("w", h)[:], B("oh", h)[:], A[:, :, 0:16], OP.mult, 128, r=[x("oh")], w=[x("w")], pr=[ak], name="w")
+            vop(lambda v, h=h: v.tensor_tensor_scan(B("RM", h)[:], T.NF[:], B("w", h)[:], 0.0, OP.mult, OP.add), 128, r=[W("NF"), x("w")], w=[x("RM")], name="RW")
+            spread(h, B("RM", h), x("RM"), B("brep", h), x("brep"))
+            tt(B("nm", h)[:], B("brep", h)[:], A[:, :, 0:16], OP.not_equal, 128, r=[x("brep")], w=[x("nm")], pr=[ak], name="nm")
+            mm(C[:, :, 48:64], B("nm", h)[:], T.I3072[:], True, True, ck, 128, r=[x("nm"), W("I3072")], name="LMn")
+            tt(B("LMf", h)[:], T.O[:, hs(h)], C[:, :, 48:64], OP.add, 128, r=[oreg(h)], w=[x("LMf")], pr=[ck], name="LMf")
+            cpv(T.LM[:, S(h)], B("LMf", h)[:], 128, r=[x("LMf")], w=[x("LM")], name="LM")
+            flex(B("XM", h)[:], T.XX[:].indirect(T.LM[:, S(h)]), 2048, r=[W("XX"), x("LM")], w=[x("XM")], cyc=GCY, name="XM%d" % h)
+            tt(B("BD", h)[:], B("brep", h)[:], T.QM[:, 0:128], OP.mult, 128, r=[x("brep"), W("QM")], w=[x("BD")], name="BD")
+            mm(A[:, :, 56], B("BD", h)[:], T.U8[:], True, True, ak, 8, r=[x("BD"), W("U8")], f32=True, name="LBp")
+            cpv(T.LB[:, 8 * h:8 * h + 8], A[:, :, 56], 8, w=[("LB", 8 * h, 8 * h + 8)], pr=[ak], name="LB")
+            flex(B("XB", h)[:], T.XX[:, 0:V_].indirect(T.LB[:, 8 * h:8 * h + 8]), 128, r=XR + [("LB", 8 * h, 8 * h + 8)], w=[x("XB")], cyc=GCY, name="XB%d" % h)
+            if h not in MXS: mm(C[:, :, 32:48], T.Ib[:], B("XB", h)[:], True, True, ck, 128, r=[x("XB")], name="XBp")
+        for h in H:
+            A, C, Bk = P("A", h), P("C", h), P("B", h); ak, ck, bk = "pA%d" % h, "pC%d" % h, "pB%d" % h
+            x = lambda n: W(n + str(h))
+            mm(A[:, :, 40:56], B("cS", h)[:], T.If[:], True, True, ak, 128, r=[x("cS"), W("If")], f32=True, name="cK")
+            tt(B("cKv", h)[:], A[:, :, 40:56], VR[:, S(h)], OP.subtract, 128, r=[W("VR%d" % t)], w=[x("cKv")], pr=[ak], name="cKv")
+            MX = B("MX", h)
+            if h in MXS:
+                for c in range(4):
+                    bn = ck if c % 2 else "pE"
+                    for kk in range(4):
+                        o = C[:, :, 16 * kk:16 * kk + 16] if c % 2 else T.pE[:, S(kk)]
+                        mm(o, T.Ib[:], B("XK", h)[:, 4 * c + kk::16], True, False, bn, 128, r=[x("XK")], name="DF")
+                        mm(o, T.Im[:], B("XB", h)[:], False, True, bn, 128, r=[x("XB")], name="DF")
+                    act(MX[:, c], C[:] if c % 2 else T.pE[:], 512, ActivationFunctionType.Abs, w=[("MX%d" % h, 4 * c, 4 * c + 4)], pr=[bn], name="MXa")
+            else:
+                for k in range(16):
+                    tt(MX[:, k // 4, 2 * (k % 4):2 * (k % 4) + 2], B("XK", h)[:, k::16], C[:, :, 32:48], OP.max, 128, r=[x("XK")], w=[("MX%d" % h, k, k + 1)], pr=[ck], name="MX")
+            mm(A[:, :, 24:40], T.Ib[:], T.K2[:], True, False, ak, 128, r=[W("Ib"), W("K2")], name="FL")
+            for k in range(16):
+                c, kk = divmod(k, 4)
+                mr = [("MX%d" % h, k, k + 1)]
+                if h in MXS:
+                    l = MX[:, c, :, 16 * kk:16 * kk + 16] if c % 2 else MX[:, c, 2 * kk:2 * kk + 2]
+                    mm(A[:, :, 24 + k], l, T.S16[:], False, k == 15, ak, 8, r=mr + [W("S16")], name="FL")
+                else:
+                    mm(A[:, :, 24 + k], B("XK", h)[:, k::16], T.Sm16[:], False, False, ak, 8, r=[x("XK"), W("Sm16")], name="FL")
+                    mm(A[:, :, 24 + k], MX[:, c, 2 * kk:2 * kk + 2], T.S32[:], False, k == 15, ak, 8, r=mr + [W("S32")], name="FL")
+            for k in range(16):
+                mm(Bk[:, :, 24 + k], B("ST", h)[:, k::16], T.S1[:], True, True, bk, 8, r=[x("ST"), W("S1")], name="SL")
+            tt(Bk[:, :, 0:16], B("nm", h)[:], Bk[:, :, 24:40], OP.min, 128, r=[x("nm")], pr=[bk], pw=[bk], name="el")
+            mm(C[:, :, 0:16], B("brep", h)[:], T.If[:], True, True, ck, 128, r=[x("brep"), W("If")], f32=True, name="bR")
+            tt(T.aD[:, S(h)], T.O[:, hs(h)], T.DM[:, S(h)], OP.subtract, 128, r=[oreg(h), W("DM")], w=[("aD", 128 * h, 128 * h + 128)], name="aD")
+            act(C[:, :, 16:32], B("brep", h)[:], 128, IDENT, bias=T.VC[:, 8 + 2 * t + h:9 + 2 * t + h], r=[x("brep"), W("VC")], pw=[ck], name="bmv")
+        for h in H:
+            Bk = P("B", h); bk = "pB%d" % h
+            x = lambda n: W(n + str(h))
+            ws = T.pD[:, :, 16 * h:16 * h + 16]
+            for k in range(16):
+                mm(ws, T.Ib[:], B("XM", h)[:, k::16], k == 0, k == 15, "pD", 128, r=[x("XM")], name="WS")
+            ts(B("wp", h)[:], ws, 0.0, OP.is_gt, 128, w=[x("wp")], pr=["pD"], name="wp")
+            mm(Bk[:, :, 40:56], B("wp", h)[:], T.BOb[:], True, True, bk, 128, r=[x("wp"), W("BOb")], name="WN")
+            ts(B("win", h)[:], Bk[:, :, 40:56], T.Zc[:, 0:1], OP.is_ge, 128, r=[W("Zc")], w=[x("win")], pr=[bk], name="win")
+            tt(B("nC0", h)[:], B("win", h)[:], P("C", h)[:, :, 16:32], OP.mult, 128, r=[x("win")], w=[x("nC0")], pr=["pC%d" % h], name="nC0")
+            ts(B("nC", h)[:], B("nC0", h)[:], T.VC[:, 2 * t + h:2 * t + h + 1], OP.add, 128, r=[x("nC0"), W("VC")], w=[x("nC")], name="nC")
+            if not last:
+                SN = T.SND[:, t]; sr = lambda o: ("SND%d" % t, 2 * h + o, 2 * h + o + 1)
+                cpv(SN[:, h, :, 0], B("nC", h)[:, 0::16], 8, r=[x("nC")], w=[sr(0)], name="hi")
+                tt(SN[:, h, :, 1], B("nC", h)[:, 0::16], SN[:, h, :, 0], OP.subtract, 8, r=[x("nC"), sr(0)], w=[sr(1)], name="lo")
+        if not last:
+            ds = [D_OF[u] for u in range(t + 1, RO)]
+            land = LU(t + 1, rank); sem = "ar%d_%d" % (t + 1, rank)
+            sa = send([T.cores[(rank - ds[0]) % NR]], T.SND[:, t], land, sem, [W("SND%d" % t)], 8, "send")
+            sb_ = send([T.cores[(rank - q) % NR] for q in ds[1:]], T.SND[:, t], land, sem, [W("SND%d" % t)], 8, "sendb") if len(ds) > 1 else None
+        for h in H:
+            A, Bk, C = P("A", h), P("B", h), P("C", h); ak, bk, ck = "pA%d" % h, "pB%d" % h, "pC%d" % h
+            x = lambda n: W(n + str(h))
+            tt(B("ew", h)[:], B("win", h)[:], Bk[:, :, 0:16], OP.mult, 128, r=[x("win")], w=[x("ew")], pr=[bk], name="ew")
+            tt(B("q2", h)[:], B("ew", h)[:], A[:, :, 24:40], OP.mult, 128, r=[x("ew")], w=[x("q2")], pr=[ak], name="q2")
+            vop(lambda v, h=h: v.tensor_tensor_scan(B("RM", h)[:], T.NF[:], B("q2", h)[:], 0.0, OP.mult, OP.max), 128, r=[W("NF"), x("q2")], w=[x("RM")], name="RM2")
+            best = T.pE[:, 256 + 128 * h:384 + 128 * h]
+            spread(h, B("RM", h), x("RM"), best, None, floor=0.5, bank="pE")
+            tt(B("oh2_", h)[:], B("q2", h)[:], best, OP.is_equal, 128, r=[x("q2")], w=[x("oh2_")], pr=["pE"], name="oh2")
+            mm(Bk[:, :, 0:16], B("oh2_", h)[:], T.Ib[:], True, True, bk, 128, r=[x("oh2_")], name="oh2T")
+            tt(B("pz", h)[:], T.aD[:, S(h)], Bk[:, :, 0:16], OP.mult, 128, r=[("aD", 128 * h, 128 * h + 128)], w=[x("pz")], pr=[bk], name="pz")
+            tt(B("pc", h)[:], B("cKv", h)[:], Bk[:, :, 0:16], OP.mult, 128, r=[x("cKv")], w=[x("pc")], pr=[bk], name="pc")
+            hr = lambda n: (n, 128 * h, 128 * h + 128)
+            act(T.oK[:, S(h)], Bk[:, :, 0:16], 128, w=[hr("oK")], pr=[bk], name="oK")
+            act(C[:, :, 32:48], Bk[:, :, 0:16], 128, COPY, bias=1.0, scale=-1.0, pr=[bk], pw=[ck], name="nk")
+            zm = T.pD[:, :, 32 + 16 * h:48 + 16 * h]
+            mm(zm, T.ONE[:], T.DR[:, S(h)], True, False, "pD", 128, r=[W("ONE"), W("DR")], name="zm")
+            mm(zm, T.BOf[:], B("pz", h)[:], False, True, "pD", 128, r=[W("BOf"), x("pz")], f32=True, name="zm")
+            tt(T.ZQ[:, S(h)], T.QM[:, S(h)], zm, OP.mult, 128, r=[W("QM")], w=[hr("ZQ")], pr=["pD"], name="ZQ")
+            cpv(T.ZU[:, S(h)], zm, 128, w=[hr("ZU")], pr=["pD"], name="ZU")
+            vop(lambda v, h=h: v.tensor_tensor_scan(T.ZS[:, S(h)], T.NF[:], T.ZQ[:, S(h)], 0.0, OP.mult, OP.add), 128, r=[W("NF"), hr("ZQ")], w=[hr("ZS")], name="ZS")
+            zl = ("ZL", 8 * h, 8 * h + 8)
+            cpv(T.ZL[:, 8 * h:8 * h + 8], T.ZS[:, 128 * h + 15:128 * h + 128:16], 8, r=[hr("ZS")], w=[zl], name="ZL")
+            mm(T.pD[:, :, 16 * h:16 * h + 16], T.BOf[:], B("pc", h)[:], True, True, "pD", 128, r=[x("pc")], f32=True, name="csv")
+            flex(B("OC", h)[:], T.O[:].indirect(T.ZL[:, 8 * h:8 * h + 8]), 128, r=[W("O"), zl], w=[x("OC")], cyc=GCY, name="OC", only="S")
+            vop(lambda v, h=h, VR=VR: v.tensor_tensor(B("OE", h)[:], T.O[:].indirect(T.ZL[:, 8 * h:8 * h + 8]), VR[:, S(h)], OP.is_equal), 128, r=[W("O"), zl, W("VR%d" % t)], w=[x("OE")], two=GCY, name="OE")
+            tt(C[:, :, 48:64], T.oK[:, S(h)], C[:, :, 0:16], OP.mult, 128, r=[hr("oK")], pr=[ck], pw=[ck], name="hb")
+        for h in H:
+            x = lambda n: W(n + str(h)); hr = lambda n: (n, 128 * h, 128 * h + 128)
+            n1 = T.pD[:, :, 16 * h:16 * h + 16]
+            tt(n1, B("OE", h)[:], n1, OP.mult, 128, r=[x("OE")], pr=["pD"], pw=["pD"], name="n1")
+            tt(T.NC[:, S(h)], B("OC", h)[:], n1, OP.add, 128, r=[x("OC")], w=[hr("NC")], pr=["pD"], name="NC")
+        for u in range(16):
+            ts(T.DE[:, 256 * u + 16 * u:256 * u + 256], T.ZU[:, 16 * u:256], T.ZS[:, 16 * u + 15:16 * u + 16], OP.is_equal, 256 - 16 * u,
+               r=[("ZU", 16 * u, 256), ("ZS", 16 * u, 16 * u + 16)], w=[("DE", 256 * u, 256 * u + 256)], two=0.5, name="DE")
+        mm(T.pE[:, 0:256], T.Ib[:], T.DC[:], True, False, "pE", 256, r=[W("Ib"), W("DC")], name="DUP")
+        for u in range(16):
+            dr = [("DE", 256 * u, 256 * u + 256)]
+            mm(T.pE[:, 16 * u:16 * u + 16], T.LW[:], T.DE[:, 272 * u:272 * u + 16], False, u == 15, "pE", 16, r=dr + [W("LW")], name="DUP")
+            if u < 15: mm(T.pE[:, 16 * u + 16:256], T.L4[:], T.DE[:, 272 * u + 16:256 * u + 256], False, False, "pE", 240 - 16 * u, r=dr + [W("L4")], name="DUP")
+        vop(lambda v: v.tensor_scalar(T.pE[:, 0:256], T.pE[:, 0:256], 0.0, 8192.0, OP.is_ge, OP.mult), 256, pr=["pE"], pw=["pE"], name="nlq")
+        tt(T.fz[:], T.ZQ[:], T.pE[:, 0:256], OP.max, 256, r=[W("ZQ")], w=[W("fz")], pr=["pE"], name="fz")
+        for h in H:
+            vop(lambda v, h=h: v.tensor_tensor_scan(T.FS[:, S(h)], T.NF[:], T.fz[:, S(h)], 0.0, OP.mult, OP.add), 128, r=[W("NF"), ("fz", 128 * h, 128 * h + 128)], w=[("FS", 128 * h, 128 * h + 128)], name="FS")
+        tt(T.fl[:], T.FS[:, 15::16], T.DL[:], OP.min, 16, r=[W("FS"), W("DL")], w=[W("fl")], name="fl")
+        cpv(T.FZ[:], T.fl[:], 16, r=[W("fl")], w=[W("FZ")], name="FZ")
+        vop(lambda v: v.tensor_copy(T.O[:].indirect(T.FZ[:]), T.NC[:]), 256, r=[W("NC"), W("FZ")], w=[W("O")], two=3.0, name="scatter")
+        G["wr"]["O"] = [y for y in G["wr"]["O"]]
+        for h in H:
+            hr = lambda n: (n, 128 * h, 128 * h + 128)
+            ck = "pC%d" % h
+            tt(T.XO[:, S(h)], T.O[:, hs(h)], P("C", h)[:, :, 32:48], OP.mult, 128, r=[oreg(h)], w=[hr("XO")], pr=[ck], name="XO")
+            tt(T.O[:, hs(h)], T.XO[:, S(h)], P("C", h)[:, :, 48:64], OP.add, 128, r=[hr("XO")], w=[("O", 1536 * h, 1536 * h + 1536)], pr=[ck], name="O")
+        for h in H:
+            x = lambda n: W(n + str(h)); ck = "pA%d" % h; C = P("A", h)
+            cr = lambda n: (n, 96 * h, 96 * h + 96)
+            tt(T.CLk[:, 96 * h:96 * h + 96], T.CLf[:, 96 * h:96 * h + 96], T.KP[:, t], OP.mult, 96, r=[cr("CLf"), W("KP%d" % t)], w=[cr("CLk")], name="CLk")
+            tt(B("BDc", h)[:], B("nC", h)[:], T.PM[:, t], OP.mult, 128, r=[x("nC"), W("PM%d" % t)], w=[x("BDc")], name="BDc")
+            mm(C[:, :, 0:12], B("BDc", h)[:], T.U4[:], True, True, ck, 96, r=[x("BDc"), W("U4")], f32=True, name="CLp")
+            tt(T.CLf[:, 96 * h:96 * h + 96], T.CLk[:, 96 * h:96 * h + 96], C[:, :, 0:12], OP.add, 96, r=[cr("CLk")], w=[cr("CLf")], pr=[ck], name="CLf")
+            if not last: cpv(T.CLu[:, 96 * h:96 * h + 96], T.CLf[:, 96 * h:96 * h + 96], 96, r=[cr("CLf")], w=[cr("CLu")], name="CLu")
+        if last: break
+        for h in H:
+            mm(T.pA1[:, :, 58], T.ONE[:], B("win", h)[:, 0::16], h == 0, h == 1, "pA1", 8, r=[W("win%d" % h), W("ONE")], name="ZC")
+        vop(lambda v: v.tensor_reduce(T.zr[:, 0:1], T.pA1[:, :, 58], AxisListType.X, OP.add), 8, w=[("zr", 0, 1)], pr=["pA1"], name="zr")
+        cpv(T.zi[:, 0:1], T.zr[:, 0:1], 1, r=[("zr", 0, 1)], w=[("zi", 0, 1)])
+        ts(T.zi[:, 1:2], T.zi[:, 0:1], 1, OP.bitwise_and, 1, r=[("zi", 0, 1)], w=[("zi", 1, 2)])
+        ts(T.Zc[:], T.zi[:, 1:2], 9.0, OP.add, 1, r=[("zi", 1, 2)], w=[W("Zc")], name="Zc")
+        for qi, q in enumerate(ds):
+            s = (rank + q) % NR; ln = "L%d_%d" % (t + 1, s)
+            arrive(s, t + 1, sa if qi == 0 else sb_, 8)
+            for h in H:
+                A = P("A", h); ak = "pA%d" % h
+                flex(B("HLz", h)[:, :, 0:2], LU(t + 1, s)[:, h], 16, r=[W(ln)], w=[W("HLz%d" % h)], name="HLz")
+                mm(A[:, :, 40:56], B("HLz", h)[:], T.Ib[:], True, True, ak, 128, r=[W("HLz%d" % h)], name="HLr")
+                flex(T["WC%d" % q][:, hs(h)], A[:, :, 40:56], 128, w=[("WC%d" % q, 1536 * h, 1536 * h + 1536)], pr=[ak], name="WCu")
+    vop(lambda v: v.transpose(T.TF[:], T.CLf[:]), 192, r=[W("CLf")], w=[W("TF")], name="yc")
+    for e in range(2):
+        for b in range(6):
+            dma(T.yc[e::2, 512 * b:512 * b + 512], T.TF[:, 32 * b + 16 * e:32 * b + 16 * e + 16], 8, r=[W("TF")], name="st yc")
+    dma(T.yo[:, 0:1536], T.O[:, 0:1536], 786, r=[("O", 0, 1536)], name="st yo")
+    dma(T.yo[:, 1536:3072], T.O[:, 1536:3072], 786, r=[("O", 1536, 3072)], q="S", name="st yo")
+    return G
+
+
+ORDER = {}
+
+
+def rank_program(g, core, T, topo):
+    rank = T.rank_of(core)
+    if rank is None:
+        return
+    G = build(core, T, topo, rank)
+    if "o" not in ORDER: ORDER["o"] = schedule(G)
+    order, eng, fin, st = ORDER["o"]
+    Q = {"V": g.vector, "S": g.scalar, "P": g.tensor, "G": g, "Y": g.sync}
+    ops = G["ops"]
+    count = {}; known = {"V": {}, "S": {}, "P": {}, "G": {}, "Y": {}}; done = [None] * len(ops); clock = [None] * len(ops)
+    for i in order:
+        o = ops[i]; e = eng[i]
+        if e not in Q:
+            done[i] = (o["key"], o["cnt"]); clock[i] = {}
+            continue
+        kn = known[e]
+        need = {}
+        for j, raw in o["deps"].items():
+            if eng[j] == e and not raw: continue
+            k, c = done[j]
+            if kn.get(k, 0) < c: need[k] = max(need.get(k, 0), c)
+        cand = sorted(need.items())
+        for j in o["deps"]:
+            if eng[j] == e and not o["deps"][j]: continue
+        for k, c in cand:
+            if kn.get(k, 0) >= c: continue
+            Q[e].wait_ge(T.sem[k], c)
+            kn[k] = max(kn.get(k, 0), c)
+            for j in o["deps"]:
+                if done[j] == (k, c):
+                    for kk, vv in clock[j].items(): kn[kk] = max(kn.get(kk, 0), vv)
+        ins = o["fn"](Q, e)
+        if o["key"] is None:
+            k = "c" + e
+            count[k] = count.get(k, 0) + 1
+            ins.then_inc(T.sem[k], 1)
+            done[i] = (k, count[k])
+        else:
+            k = o["key"]
+            count[k] = count.get(k, 0) + o["cnt"]
+            done[i] = (k, count[k])
+        c = dict(kn); c[done[i][0]] = max(c.get(done[i][0], 0), done[i][1])
+        clock[i] = c
+    for k in sorted(count): g.wait_ge(T.sem[k], count[k])

@@ -25,15 +25,16 @@ def _decl():
     sb("VC", [128, 16], f)
     for n in ("XK", "CG", "ST", "MN", "XM"): sb(n, [128, 2, 2048], b)
     sb("MX", [128, 2, 4, 8, 64], b); sb("E", [128, 2, 8, 8, 16], b); sb("PR", [128, 2, 15, 8, 16], b)
-    for n in ("cS", "RM", "BR", "oh", "w", "brep", "LMf", "BD", "cKv", "q2", "pz", "pc", "nC0", "nC", "BDc", "OC", "OE"): sb(n, [128, 2, 128], f)
-    for n in ("nm", "XB", "wp", "win", "ew", "oh2_"): sb(n, [128, 2, 128], b)
+    for n in ("cS", "RM", "BR", "oh", "w", "brep", "BD", "cKv", "q2", "pz", "pc", "nC0", "nC", "BDc", "OC", "OE"): sb(n, [128, 2, 128], f)
+    for n in ("nm", "XB", "SX", "wp", "win", "el", "oh2_"): sb(n, [128, 2, 128], b)
     sb("mS", [128, 2, 8, 24], b); sb("LM", [128, 256], u); sb("BZ", [128, 2, 128], f); sb("kS", [128, 2, 128], f); sb("HLz", [128, 2, 8, 16], b)
     sb("LA", [128, 256], u); sb("LB", [128, 16], u); sb("ZL", [128, 16], u); sb("FZ", [128, 16], u); sb("ZU", [128, 256], u)
-    for n in ("aD", "oK", "ZQ", "ZS", "NC", "nlq", "fz", "FS", "XO", "DM", "QM"): sb(n, [128, 256], f)
+    for n in ("aD", "ZQ", "ZS", "NC", "nlq", "fz", "FS", "XO", "QM"): sb(n, [128, 256], f)
     sb("fl", [128, 16], f); sb("DL", [128, 16], f); sb("DE", [128, 4096], b)
-    for n in ("Ib", "Im", "I256", "I16", "I3072", "BOb", "L4", "LW", "ONE", "K1", "K2"): sb(n, [128, 128], b)
+    for n in ("Ib", "Im", "Im16", "I256", "I16", "I3072", "BOb", "BN", "L4", "LW", "ONE", "K1", "K2"): sb(n, [128, 128], b)
     for n in ("If", "BOf", "NF"): sb(n, [128, 128], f)
-    for n in ("DC", "DR"): sb(n, [128, 256], b)
+    for n in ("DC", "C128", "oK"): sb(n, [128, 256], b)
+    for n in ("VH", "VL"): sb(n, [128, 4, 256], b)
     for n in ("S1", "S16", "S32", "Sm16", "SHL"): sb(n, [128, 8], b)
     sb("U8", [128, 8], f); sb("U4", [128, 96], f)
     sb("ci", [128, 256], f); sb("cg", [128, 256], f); sb("cq", [128, 256], f)
@@ -51,7 +52,9 @@ D_OF = [1 + t % 3 for t in range(RO)]
 CYC = 0.83e-3
 WAKE = 0.09
 GCY = 1.5
-ASG = {"XK0": "S", "XK1": "S", "CG0": "S", "CG1": "S", "XM0": "S", "XM1": "S"}
+ASG = {"XK1": "S", "CG0": "S", "CG1": "S", "XM0": "S", "XM1": "S", "compose0": "S", "compose1": "S", "compose2": "S", "compose3": "S"}
+NPC, NPM, NPS = 2, 2, 8
+WT = {'ST': -10, 'SX': -5, 'zr': -10, 'key': 10, 'XB1': 10, 'RW': 20, 'BDc': -10, 'LM': -10, 'LA': 2, 'compose1': 10, 'RM': 2, 'pc': -10, 'pz': -5, 'ld sha': 10, 'el': -20, 'q2': 20, 'cL': 20, 'ZQ': -20, 'ext': -5, 'win': -2, 'oh2T': 10, 'CLu': -10, 'mS': 10, 'HLz': 2, 'oh2': 10, 'VT': -10, 'XM0': -2, 'csv': -2, 'flat': -2, 'CLk': 5, 'nk': 2, 'ZU': 10, 'Zc': -2, 'LMa': 20, 'CLf': -20, 'OC': 10, 'ld ctl': 5, 'nlq': 20, 'ld list': 20, 'send': 20, 'nC0': 10, 'hb': 2, 'bmv': 2, 'lo': 2, 'ld hol': 10, 'a1': 10, 'CF': -5, 'sendb': 5, 'zm': 20, 'fl': -2, 'OE': 20, 'DUP1': -5, 'FZ': -5, 'nC': 2, 'RM2': -20, 'sp': 10, 'scatter': 5, 'SXc': -10, 'WCu': -10, 'wp': 10, 'cKv': -2, 'XO': -2, 'compose3': 10, 'st yo': 5, 'hi': 5, 'O': 5}
 MXS = ()
 PRS = ()
 
@@ -91,7 +94,7 @@ def add(G, opts, fn, r=(), w=(), pr=(), pw=(), key=None, cnt=1, name=""):
     return n
 
 
-def schedule(G, wake=WAKE, quant=0.12):
+def schedule(G, wake=WAKE, quant=0.08):
     ops = G["ops"]; n = len(ops)
     succ = [[] for _ in range(n)]; ind = [len(o["deps"]) for o in ops]
     for i, o in enumerate(ops):
@@ -100,6 +103,7 @@ def schedule(G, wake=WAKE, quant=0.12):
     for i in range(n - 1, -1, -1):
         d = min(x[1] for x in ops[i]["opts"].values())
         prio[i] = d + max([prio[s] + 0.5 * wake for s in succ[i]] or [0.0])
+    prio = [p + WT.get(o["name"], 0.0) for p, o in zip(prio, ops)]
     free = {}; fin = [0.0] * n; eng = [None] * n; rdy = {}
     order = []; t_ready = [0.0] * n
     for i in range(n):
@@ -127,7 +131,7 @@ def schedule(G, wake=WAKE, quant=0.12):
 
 def vc(n, two=1.0): return max(64.0, n * two) * CYC * 1.2 + 0.01
 def sc(n): return max(64.0, n) * CYC * 1.2 + 0.03
-def pc_(n, f32=False): return max(64.0, n) * CYC * (4.0 if f32 else 1.0) + 0.01
+def pc_(n, f32=False): return max(64.0, n) * CYC * 1.1 * (4.0 if f32 else 1.0) + 0.01
 
 
 def build(core, T, topo, rank):
@@ -192,7 +196,9 @@ def build(core, T, topo, rank):
     H = (0, 1)
 
     def ext(X, bank):
-        add(G, {"S": (sc(64), sc(64))}, lambda Q, e: Q["S"].activation(X[:, :, 16:24], X[:, :, 0:8], COPY), (), (), (bank,), (bank,), name="ext")
+        opts = {"V": (vc(64), vc(64)), "S": (sc(64), sc(64))}
+        if "ext" in ASG: opts = {ASG["ext"]: opts[ASG["ext"]]}
+        add(G, opts, lambda Q, e: Q["V"].tensor_copy(X[:, :, 16:24], X[:, :, 0:8]) if e == "V" else Q["S"].activation(X[:, :, 16:24], X[:, :, 0:8], COPY), (), (), (bank,), (bank,), name="ext")
 
     def P(n, h): return T["p" + n + str(h)]
     def B(n, h): return T[n][:, h]
@@ -220,7 +226,6 @@ def build(core, T, topo, rank):
     gop(lambda g: g.iota(T.cg[:], [[1, 16], [0, 16]], 0, 0, allow_small_or_imprecise_dtypes=True), 256, w=[W("cg")])
     gop(lambda g: g.iota(T.cq[:], [[0, 16], [1, 16]], 0, 0, allow_small_or_imprecise_dtypes=True), 256, w=[W("cq")])
     gop(lambda g: g.iota(T.DL[:], [[16, 16]], V_, 0, allow_small_or_imprecise_dtypes=True), 16, w=[W("DL")])
-    gop(lambda g: g.iota(T.DM[:], [[1, 256]], V_, 0, allow_small_or_imprecise_dtypes=True), 256, w=[W("DM")])
     for t in range(RO):
         gop(lambda g, t=t: g.iota(T.VR[:, t], [[12, 256]], t, 0, allow_small_or_imprecise_dtypes=True), 256, w=[W("VR%d" % t)])
 
@@ -230,7 +235,13 @@ def build(core, T, topo, rank):
             G["ops"][i]["deps"][s2] = False
     vt(0)
     vt(1)
-    for d in (1, 2, 3): vop(lambda v, d=d: v.memset(T["WC%d" % d][:], 0.0), V_, w=[W("WC%d" % d)], two=0.5)
+    for t in range(RO):
+        gop(lambda g, t=t: g.iota(T.VH[:, t], [[48, 64], [0, 4]], 0, 0, allow_small_or_imprecise_dtypes=True), 256, w=[W("VH%d" % t)])
+        gop(lambda g, t=t: g.iota(T.VL[:, t], [[0, 64], [12, 4]], t, 0, allow_small_or_imprecise_dtypes=True), 256, w=[W("VL%d" % t)])
+    vop(lambda v: v.memset(T.WC1[:], 0.0), V_, w=[W("WC1")], two=0.5)
+    for d in (2, 3):
+        i = gop(lambda g, d=d: g.iota(T["WC%d" % d][:], [[0, V_]], 0, 0, allow_small_or_imprecise_dtypes=True), V_, w=[W("WC%d" % d)])
+        G["ops"][i]["deps"][s2] = False
     for d in (1, 2, 3):
         s = (rank + d) % NR
         arrive(s, 0, s1 if d == D_OF[0] else s2, 98 if d == D_OF[0] else 196)
@@ -260,14 +271,12 @@ def build(core, T, topo, rank):
     ts(T.DL[:], T.DL[:], F(2), OP.add, 16, r=tfr + [W("DL")], w=[W("DL")])
     ci = T.ci[:, 0:128]; rc = tfr + [W("ci")]; rq = tfr + [W("cq")]; rg = tfr + [W("cg")]
     ts(T.If[:], ci, F(0), OP.is_equal, 128, r=rc, w=[W("If")])
-    for nmx, s in (("Ib", 1.0), ("Im", -1.0), ("I256", -256.0), ("I16", 16.0), ("I3072", 3072.0)):
-        ts(T[nmx][:], ci, F(0), OP.is_equal, 128, r=rc, w=[W(nmx)], s2=s, op1=OP.mult)
     ts(T.BOf[:], T.cg[:, 0:128], F(1), OP.is_equal, 128, r=rg, w=[W("BOf")])
-    for nmx, s in (("BOb", 1.0), ("L4", 4.0)):
-        ts(T[nmx][:], T.cg[:, 0:128], F(1), OP.is_equal, 128, r=rg, w=[W(nmx)], s2=s, op1=OP.mult)
+    for src, nmx, s in (("If", "Ib", 1.0), ("If", "Im", -1.0), ("If", "Im16", -16.0), ("If", "I16", 16.0), ("If", "I3072", 3072.0), ("BOf", "BOb", 1.0), ("BOf", "L4", 4.0), ("BOf", "BN", -128.0)):
+        act(T[nmx][:], T[src][:], 128, COPY, scale=s, r=[W(src)], w=[W(nmx)])
     ts(T.QM[:], T.cq[:], F(2), OP.is_equal, 256, r=rq, w=[W("QM")])
     ts(T.NF[:], T.cq[:, 0:128], 0.0, OP.not_equal, 128, r=[W("cq")], w=[W("NF")])
-    for nmx, s in (("S1", 1.0), ("S16", 16.0), ("S32", 32.0), ("Sm16", -16.0)):
+    for nmx, s in (("S1", 1.0), ("S16", 16.0), ("S32", 32.0)):
         ts(T[nmx][:], T.ci[:, 0:8], F(1), OP.is_equal, 8, r=rc, w=[W(nmx)], s2=s, op1=OP.mult)
     ts(T.wq[:, 0:1], F(2), 1.0, OP.is_le, 1, r=tfr, w=[("wq", 0, 1)])
     ts(T.SHL[:], T.ci[:, 0:8], F(1), OP.is_equal, 8, r=rc + [("wq", 0, 1)], w=[W("SHL")], s2=T.wq[:, 0:1], op1=OP.mult)
@@ -281,12 +290,11 @@ def build(core, T, topo, rank):
     tt(T.FS[:], T.fz[:], T.QM[:], OP.mult, 256, r=[W("fz"), W("QM")], w=[W("FS")])
     vop(lambda v: v.tensor_reduce(T.wq[:, 1:2], T.FS[:, 0:16], AxisListType.X, OP.add), 16, r=[W("FS")], w=[("wq", 1, 2)])
     ts(T.LW[:], T.BOf[:], T.wq[:, 1:2], OP.mult, 128, r=[W("BOf"), ("wq", 1, 2)], w=[W("LW")])
-    ts(T.nlq[:], T.QM[:], 64.0, OP.mult, 256, r=[W("QM")], w=[W("nlq")], s2=-64.0, op1=OP.add)
+    ts(T.nlq[:], T.QM[:], 1024.0, OP.mult, 256, r=[W("QM")], w=[W("nlq")], s2=-1024.0, op1=OP.add)
+    act(T.C128[:], T.QM[:], 256, COPY, scale=128.0, r=[W("QM")], w=[W("C128")])
+    ts(T.DL[:], T.DL[:], 1.0, OP.add, 16, r=[W("DL")], w=[W("DL")])
     ts(T.ZQ[:], T.FS[:], -2.0, OP.mult, 256, r=[W("FS")], w=[W("ZQ")])
     tt(T.DC[:], T.nlq[:], T.ZQ[:], OP.add, 256, r=[W("nlq"), W("ZQ")], w=[W("DC")])
-    ts(T.wq[:, 2:3], F(0), 0.0, OP.is_equal, 1, r=tfr, w=[("wq", 2, 3)], s2=float(V_), op1=OP.mult)
-    ts(T.wq[:, 3:4], F(0), 1.0, OP.is_equal, 1, r=tfr, w=[("wq", 3, 4)])
-    ts(T.DR[:], T.ci[:], T.wq[:, 3:4], OP.mult, 256, r=[W("ci"), ("wq", 2, 4)], w=[W("DR")], s2=T.wq[:, 2:3], op1=OP.add)
     vop(lambda v: v.memset(T.O[:, V_:V_ + PAD], 0.0), PAD, w=[("O", V_, V_ + PAD)])
     for h in H:
         vop(lambda v, h=h: v.memset(B("BZ", h)[:], 0.0), 128, w=[W("BZ%d" % h)])
@@ -320,11 +328,15 @@ def build(core, T, topo, rank):
         for c in range(4):
             flex(T.CC[:, 768 * c:768 * c + 768], T[wc][:].indirect(T.CLu[:, 48 * c:48 * c + 48]), 768, r=[W(wc), W("CLu")], w=[("CC", 768 * c, 768 * c + 768)], cyc=GCY, name="compose%d" % c)
         la = lambda h: ("LA", 128 * h, 128 * h + 128)
-        for h in H: flex(B("XK", h)[:], T.XX[:, 0:V_].indirect(T.LA[:, S(h)]), 2048, r=XR + [la(h)], w=[W("XK%d" % h)], cyc=GCY, name="XK%d" % h)
-        for h in H: flex(B("CG", h)[:], T.CC[:].indirect(T.LA[:, S(h)]), 2048, r=[W("CC"), la(h)], w=[W("CG%d" % h)], cyc=GCY, name="CG%d" % h)
+        pieces = lambda n: [(2048 // n * p, 2048 // n * (p + 1), 128 // n * p, 128 // n * (p + 1)) for p in range(n)]
         for h in H:
-            vop(lambda v, h=h, VT=VT: v.tensor_tensor(B("ST", h)[:], T.O[:, 0:V_].indirect(T.LA[:, S(h)]), VT[:, 2048 * h:2048 * h + 2048], OP.is_equal), 2048,
-                r=[("O", 0, V_), la(h), ("VT%d" % (t % 2), 2048 * h, 2048 * h + 2048)], w=[W("ST%d" % h)], two=GCY, name="ST")
+            for a, z, c, e in pieces(NPC): flex(B("XK", h)[:, a:z], T.XX[:, 0:V_].indirect(T.LA[:, 128 * h + c:128 * h + e]), z - a, r=XR + [la(h)], w=[("XK%d" % h, a, z)], cyc=GCY, name="XK%d" % h)
+        for h in H:
+            for a, z, c, e in pieces(NPC): flex(B("CG", h)[:, a:z], T.CC[:].indirect(T.LA[:, 128 * h + c:128 * h + e]), z - a, r=[W("CC"), la(h)], w=[("CG%d" % h, a, z)], cyc=GCY, name="CG%d" % h)
+        for h in H:
+            for a, z, c, e in pieces(NPS):
+                vop(lambda v, h=h, VT=VT, a=a, z=z, c=c, e=e: v.tensor_tensor(B("ST", h)[:, a:z], T.O[:, 0:V_].indirect(T.LA[:, 128 * h + c:128 * h + e]), VT[:, 2048 * h + a:2048 * h + z], OP.is_equal), z - a,
+                    r=[("O", 0, V_), la(h), ("VT%d" % (t % 2), 2048 * h + a, 2048 * h + z)], w=[("ST%d" % h, a, z)], two=GCY, name="ST")
         if t + 2 < RO: vt(t + 2)
         for h in H:
             mm(P("C", h)[:, :, 0:16], T.Ib[:], T.XX[:, hs(h)], True, True, "pC%d" % h, 128, r=XR + [W("Ib")])
@@ -337,6 +349,11 @@ def build(core, T, topo, rank):
             for s in range(1, 9):
                 tt(B("E", h)[:, s - 1], B("cS", h)[:], A[:, :, s:s + 16], OP.not_equal if h in PRS else OP.is_equal, 128, r=[W("cS%d" % h)], w=[("E%d" % h, s - 1, s)], pr=[bk], name="E")
         for h in H:
+            if h in MXS: continue
+            for k in range(16):
+                mm(T.pE[:, 128 * h + k:128 * h + 128:16], B("XK", h)[:, k::16], T.S1[:], True, True, "pE", 8, r=[W("XK%d" % h), W("S1")], name="SX")
+            act(B("SX", h)[:], T.pE[:, S(h)], 128, w=[W("SX%d" % h)], pr=["pE"], name="SXc")
+        for h in H:
             Bk = P("B", h); bk = "pB%d" % h
             for k in range(16):
                 tt(B("MN", h)[:, S(k)], B("XK", h)[:, k::16], P("C", h)[:, :, 0:16], OP.min, 128, r=[W("XK%d" % h)], w=[("MN%d" % h, 128 * k, 128 * k + 128)], pr=["pC%d" % h], name="MN")
@@ -344,7 +361,8 @@ def build(core, T, topo, rank):
                 mm(Bk[:, :, k], B("MN", h)[:, S(k)], T.S1[:], True, True, bk, 8, r=[("MN%d" % h, 128 * k, 128 * k + 128), W("S1")], name="mL")
             ext(Bk, bk)
             mS = B("mS", h)
-            flex(mS[:], Bk[:, :, 0:24], 192, w=[W("mS%d" % h)], pr=[bk], name="mS", only="S")
+            nx = 24 if h in PRS else 16
+            flex(mS[:, :, 0:nx], Bk[:, :, 0:nx], 8 * nx, w=[W("mS%d" % h)], pr=[bk], name="mS")
             PRh, Eh = B("PR", h), B("E", h)
             for c in range(4 if h in PRS else 0):
                 bn = "pE" if c % 2 else bk
@@ -378,7 +396,7 @@ def build(core, T, topo, rank):
         for h in H:
             A, C = P("A", h), P("C", h); ak, ck = "pA%d" % h, "pC%d" % h
             x = lambda n: W(n + str(h))
-            act(B("kS", h)[:], C[:, :, 16:32], 128, w=[x("kS")], pr=[ck], name="kS")
+            flex(B("kS", h)[:], C[:, :, 16:32], 128, w=[x("kS")], pr=[ck], name="kS")
             vop(lambda v, h=h: v.tensor_tensor_scan(B("RM", h)[:], T.NF[:], B("kS", h)[:], 0.0, OP.mult, OP.max), 128, r=[W("NF"), x("kS")], w=[x("RM")], name="RM")
             spread(h, B("RM", h), x("RM"), B("BR", h), x("BR"))
             tt(B("oh", h)[:], B("BR", h)[:], C[:, :, 16:32], OP.is_equal, 128, r=[x("BR")], w=[x("oh")], pr=[ck], name="oh")
@@ -386,10 +404,10 @@ def build(core, T, topo, rank):
             vop(lambda v, h=h: v.tensor_tensor_scan(B("RM", h)[:], T.NF[:], B("w", h)[:], 0.0, OP.mult, OP.add), 128, r=[W("NF"), x("w")], w=[x("RM")], name="RW")
             spread(h, B("RM", h), x("RM"), B("brep", h), x("brep"))
             tt(B("nm", h)[:], B("brep", h)[:], A[:, :, 0:16], OP.not_equal, 128, r=[x("brep")], w=[x("nm")], pr=[ak], name="nm")
-            mm(C[:, :, 48:64], B("nm", h)[:], T.I3072[:], True, True, ck, 128, r=[x("nm"), W("I3072")], name="LMn")
-            tt(B("LMf", h)[:], T.O[:, hs(h)], C[:, :, 48:64], OP.add, 128, r=[oreg(h)], w=[x("LMf")], pr=[ck], name="LMf")
-            cpv(T.LM[:, S(h)], B("LMf", h)[:], 128, r=[x("LMf")], w=[x("LM")], name="LM")
-            flex(B("XM", h)[:], T.XX[:].indirect(T.LM[:, S(h)]), 2048, r=[W("XX"), x("LM")], w=[x("XM")], cyc=GCY, name="XM%d" % h)
+            mm(C[:, :, 48:64], T.If[:], T.O[:, hs(h)], True, False, ck, 128, r=[oreg(h), W("If")], f32=True, name="LMa")
+            mm(C[:, :, 48:64], B("nm", h)[:], T.I3072[:], False, True, ck, 128, r=[x("nm"), W("I3072")], name="LMn")
+            cpv(T.LM[:, S(h)], C[:, :, 48:64], 128, w=[x("LM")], pr=[ck], name="LM")
+            for a, z, c, e in pieces(NPM): flex(B("XM", h)[:, a:z], T.XX[:].indirect(T.LM[:, 128 * h + c:128 * h + e]), z - a, r=[W("XX"), x("LM")], w=[("XM%d" % h, a, z)], cyc=GCY, name="XM%d" % h)
             tt(B("BD", h)[:], B("brep", h)[:], T.QM[:, 0:128], OP.mult, 128, r=[x("brep"), W("QM")], w=[x("BD")], name="BD")
             mm(A[:, :, 56], B("BD", h)[:], T.U8[:], True, True, ak, 8, r=[x("BD"), W("U8")], f32=True, name="LBp")
             cpv(T.LB[:, 8 * h:8 * h + 8], A[:, :, 56], 8, w=[("LB", 8 * h, 8 * h + 8)], pr=[ak], name="LB")
@@ -398,8 +416,10 @@ def build(core, T, topo, rank):
         for h in H:
             A, C, Bk = P("A", h), P("C", h), P("B", h); ak, ck, bk = "pA%d" % h, "pC%d" % h, "pB%d" % h
             x = lambda n: W(n + str(h))
-            mm(A[:, :, 40:56], B("cS", h)[:], T.If[:], True, True, ak, 128, r=[x("cS"), W("If")], f32=True, name="cK")
-            tt(B("cKv", h)[:], A[:, :, 40:56], VR[:, S(h)], OP.subtract, 128, r=[W("VR%d" % t)], w=[x("cKv")], pr=[ak], name="cKv")
+            mm(A[:, :, 40:56], B("cS", h)[:], T.If[:], True, False, ak, 128, r=[x("cS"), W("If")], f32=True, name="cK")
+            mm(A[:, :, 40:56], T.Im[:], T.VH[:, t, S(h)], False, False, ak, 128, r=[W("Im"), W("VH%d" % t)], name="cK")
+            mm(A[:, :, 40:56], T.Im[:], T.VL[:, t, S(h)], False, True, ak, 128, r=[W("Im"), W("VL%d" % t)], name="cK")
+            act(B("cKv", h)[:], A[:, :, 40:56], 128, w=[x("cKv")], pr=[ak], name="cKv")
             MX = B("MX", h)
             if h in MXS:
                 for c in range(4):
@@ -413,6 +433,7 @@ def build(core, T, topo, rank):
                 for k in range(16):
                     tt(MX[:, k // 4, 2 * (k % 4):2 * (k % 4) + 2], B("XK", h)[:, k::16], C[:, :, 32:48], OP.max, 128, r=[x("XK")], w=[("MX%d" % h, k, k + 1)], pr=[ck], name="MX")
             mm(A[:, :, 24:40], T.Ib[:], T.K2[:], True, False, ak, 128, r=[W("Ib"), W("K2")], name="FL")
+            if h not in MXS: mm(A[:, :, 24:40], T.Im16[:], B("SX", h)[:], False, False, ak, 128, r=[W("Im16"), x("SX")], name="FL")
             for k in range(16):
                 c, kk = divmod(k, 4)
                 mr = [("MX%d" % h, k, k + 1)]
@@ -420,23 +441,26 @@ def build(core, T, topo, rank):
                     l = MX[:, c, :, 16 * kk:16 * kk + 16] if c % 2 else MX[:, c, 2 * kk:2 * kk + 2]
                     mm(A[:, :, 24 + k], l, T.S16[:], False, k == 15, ak, 8, r=mr + [W("S16")], name="FL")
                 else:
-                    mm(A[:, :, 24 + k], B("XK", h)[:, k::16], T.Sm16[:], False, False, ak, 8, r=[x("XK"), W("Sm16")], name="FL")
                     mm(A[:, :, 24 + k], MX[:, c, 2 * kk:2 * kk + 2], T.S32[:], False, k == 15, ak, 8, r=mr + [W("S32")], name="FL")
             for k in range(16):
                 mm(Bk[:, :, 24 + k], B("ST", h)[:, k::16], T.S1[:], True, True, bk, 8, r=[x("ST"), W("S1")], name="SL")
-            tt(Bk[:, :, 0:16], B("nm", h)[:], Bk[:, :, 24:40], OP.min, 128, r=[x("nm")], pr=[bk], pw=[bk], name="el")
+            tt(B("el", h)[:], B("nm", h)[:], Bk[:, :, 24:40], OP.min, 128, r=[x("nm")], w=[x("el")], pr=[bk], name="el")
+            tt(Bk[:, :, 0:16], B("el", h)[:], A[:, :, 24:40], OP.mult, 128, r=[x("el")], pr=[ak], pw=[bk], name="q1")
             mm(C[:, :, 0:16], B("brep", h)[:], T.If[:], True, True, ck, 128, r=[x("brep"), W("If")], f32=True, name="bR")
-            tt(T.aD[:, S(h)], T.O[:, hs(h)], T.DM[:, S(h)], OP.subtract, 128, r=[oreg(h), W("DM")], w=[("aD", 128 * h, 128 * h + 128)], name="aD")
+            act(T.aD[:, S(h)], T.O[:, hs(h)], 128, COPY, bias=1.0, r=[oreg(h)], w=[("aD", 128 * h, 128 * h + 128)], name="a1")
             act(C[:, :, 16:32], B("brep", h)[:], 128, IDENT, bias=T.VC[:, 8 + 2 * t + h:9 + 2 * t + h], r=[x("brep"), W("VC")], pw=[ck], name="bmv")
         for h in H:
             Bk = P("B", h); bk = "pB%d" % h
             x = lambda n: W(n + str(h))
             ws = T.pD[:, :, 16 * h:16 * h + 16]
-            for k in range(16):
-                mm(ws, T.Ib[:], B("XM", h)[:, k::16], k == 0, k == 15, "pD", 128, r=[x("XM")], name="WS")
+            for p in range(NPM):
+                ln = 8 // NPM
+                for k in range(16):
+                    mm(T.pD[:, ln * p:ln * p + ln, 16 * h:16 * h + 16], T.Ib[:], B("XM", h)[:, 2048 // NPM * p + k:2048 // NPM * (p + 1):16], k == 0, k == 15, "pD", 128 // NPM, r=[("XM%d" % h, 2048 // NPM * p, 2048 // NPM * (p + 1))], name="WS")
             ts(B("wp", h)[:], ws, 0.0, OP.is_gt, 128, w=[x("wp")], pr=["pD"], name="wp")
-            mm(Bk[:, :, 40:56], B("wp", h)[:], T.BOb[:], True, True, bk, 128, r=[x("wp"), W("BOb")], name="WN")
-            ts(B("win", h)[:], Bk[:, :, 40:56], T.Zc[:, 0:1], OP.is_ge, 128, r=[W("Zc")], w=[x("win")], pr=[bk], name="win")
+            wn = T.pD[:, :, 32 + 16 * h:48 + 16 * h]
+            mm(wn, B("wp", h)[:], T.BOb[:], True, True, "pD", 128, r=[x("wp"), W("BOb")], name="WN")
+            ts(B("win", h)[:], wn, T.Zc[:, 0:1], OP.is_ge, 128, r=[W("Zc")], w=[x("win")], pr=["pD"], name="win")
             tt(B("nC0", h)[:], B("win", h)[:], P("C", h)[:, :, 16:32], OP.mult, 128, r=[x("win")], w=[x("nC0")], pr=["pC%d" % h], name="nC0")
             ts(B("nC", h)[:], B("nC0", h)[:], T.VC[:, 2 * t + h:2 * t + h + 1], OP.add, 128, r=[x("nC0"), W("VC")], w=[x("nC")], name="nC")
             if not last:
@@ -451,8 +475,7 @@ def build(core, T, topo, rank):
         for h in H:
             A, Bk, C = P("A", h), P("B", h), P("C", h); ak, bk, ck = "pA%d" % h, "pB%d" % h, "pC%d" % h
             x = lambda n: W(n + str(h))
-            tt(B("ew", h)[:], B("win", h)[:], Bk[:, :, 0:16], OP.mult, 128, r=[x("win")], w=[x("ew")], pr=[bk], name="ew")
-            tt(B("q2", h)[:], B("ew", h)[:], A[:, :, 24:40], OP.mult, 128, r=[x("ew")], w=[x("q2")], pr=[ak], name="q2")
+            tt(B("q2", h)[:], B("win", h)[:], Bk[:, :, 0:16], OP.mult, 128, r=[x("win")], w=[x("q2")], pr=[bk], name="q2")
             vop(lambda v, h=h: v.tensor_tensor_scan(B("RM", h)[:], T.NF[:], B("q2", h)[:], 0.0, OP.mult, OP.max), 128, r=[W("NF"), x("q2")], w=[x("RM")], name="RM2")
             best = T.pE[:, 256 + 128 * h:384 + 128 * h]
             spread(h, B("RM", h), x("RM"), best, None, floor=0.5, bank="pE")
@@ -464,13 +487,12 @@ def build(core, T, topo, rank):
             act(T.oK[:, S(h)], Bk[:, :, 0:16], 128, w=[hr("oK")], pr=[bk], name="oK")
             act(C[:, :, 32:48], Bk[:, :, 0:16], 128, COPY, bias=1.0, scale=-1.0, pr=[bk], pw=[ck], name="nk")
             zm = T.pD[:, :, 32 + 16 * h:48 + 16 * h]
-            mm(zm, T.ONE[:], T.DR[:, S(h)], True, False, "pD", 128, r=[W("ONE"), W("DR")], name="zm")
-            mm(zm, T.BOf[:], B("pz", h)[:], False, True, "pD", 128, r=[W("BOf"), x("pz")], f32=True, name="zm")
+            mm(zm, T.BOf[:], B("pz", h)[:], True, True, "pD", 128, r=[W("BOf"), x("pz")], f32=True, name="zm")
             tt(T.ZQ[:, S(h)], T.QM[:, S(h)], zm, OP.mult, 128, r=[W("QM")], w=[hr("ZQ")], pr=["pD"], name="ZQ")
             cpv(T.ZU[:, S(h)], zm, 128, w=[hr("ZU")], pr=["pD"], name="ZU")
             vop(lambda v, h=h: v.tensor_tensor_scan(T.ZS[:, S(h)], T.NF[:], T.ZQ[:, S(h)], 0.0, OP.mult, OP.add), 128, r=[W("NF"), hr("ZQ")], w=[hr("ZS")], name="ZS")
             zl = ("ZL", 8 * h, 8 * h + 8)
-            cpv(T.ZL[:, 8 * h:8 * h + 8], T.ZS[:, 128 * h + 15:128 * h + 128:16], 8, r=[hr("ZS")], w=[zl], name="ZL")
+            ts(T.ZL[:, 8 * h:8 * h + 8], T.ZS[:, 128 * h + 15:128 * h + 128:16], -1.0, OP.add, 8, r=[hr("ZS")], w=[zl], s2=0.0, op1=OP.max, name="ZL")
             mm(T.pD[:, :, 16 * h:16 * h + 16], T.BOf[:], B("pc", h)[:], True, True, "pD", 128, r=[x("pc")], f32=True, name="csv")
             flex(B("OC", h)[:], T.O[:].indirect(T.ZL[:, 8 * h:8 * h + 8]), 128, r=[W("O"), zl], w=[x("OC")], cyc=GCY, name="OC", only="S")
             vop(lambda v, h=h, VR=VR: v.tensor_tensor(B("OE", h)[:], T.O[:].indirect(T.ZL[:, 8 * h:8 * h + 8]), VR[:, S(h)], OP.is_equal), 128, r=[W("O"), zl, W("VR%d" % t)], w=[x("OE")], two=GCY, name="OE")
@@ -480,20 +502,31 @@ def build(core, T, topo, rank):
             n1 = T.pD[:, :, 16 * h:16 * h + 16]
             tt(n1, B("OE", h)[:], n1, OP.mult, 128, r=[x("OE")], pr=["pD"], pw=["pD"], name="n1")
             tt(T.NC[:, S(h)], B("OC", h)[:], n1, OP.add, 128, r=[x("OC")], w=[hr("NC")], pr=["pD"], name="NC")
-        for u in range(16):
-            ts(T.DE[:, 256 * u + 16 * u:256 * u + 256], T.ZU[:, 16 * u:256], T.ZS[:, 16 * u + 15:16 * u + 16], OP.is_equal, 256 - 16 * u,
-               r=[("ZU", 16 * u, 256), ("ZS", 16 * u, 16 * u + 16)], w=[("DE", 256 * u, 256 * u + 256)], two=0.5, name="DE")
-        mm(T.pE[:, 0:256], T.Ib[:], T.DC[:], True, False, "pE", 256, r=[W("Ib"), W("DC")], name="DUP")
-        for u in range(16):
-            dr = [("DE", 256 * u, 256 * u + 256)]
-            mm(T.pE[:, 16 * u:16 * u + 16], T.LW[:], T.DE[:, 272 * u:272 * u + 16], False, u == 15, "pE", 16, r=dr + [W("LW")], name="DUP")
-            if u < 15: mm(T.pE[:, 16 * u + 16:256], T.L4[:], T.DE[:, 272 * u + 16:256 * u + 256], False, False, "pE", 240 - 16 * u, r=dr + [W("L4")], name="DUP")
+        def de(u, a, z):
+            ts(T.DE[:, 256 * u + a:256 * u + z], T.ZU[:, a:z], T.ZS[:, 16 * u + 15:16 * u + 16], OP.is_equal, z - a,
+               r=[("ZU", a, z), ("ZS", 16 * u, 16 * u + 16)], w=[("DE", 256 * u + a, 256 * u + z)], two=0.5, name="DE")
+
+        def dup(h, u, a, z, wt, stop=False):
+            mm(T.pE[:, a:z], T[wt][:], T.DE[:, 256 * u + a:256 * u + z], False, stop, "pE", z - a, r=[("DE", 256 * u + a, 256 * u + z), W(wt)], name="DUP%d" % h)
+        for h in H:
+            hr = ("oK", 128 * h, 128 * h + 128)
+            mm(T.pE[:, S(h)], T.Ib[:], T.DC[:, S(h)], True, False, "pE", 128, r=[W("Ib"), W("DC")], name="DUP%d" % h)
+            mm(T.pE[:, S(h)], T.Ib[:], T.C128[:, S(h)], False, False, "pE", 128, r=[W("C128")], name="DUP%d" % h)
+            mm(T.pE[:, S(h)], T.BN[:], T.oK[:, S(h)], False, False, "pE", 128, r=[W("BN"), hr], name="DUP%d" % h)
+            for u in range(8 * h + 8):
+                if u < 8 * h:
+                    de(u, 128, 256)
+                    dup(h, u, 128, 256, "L4")
+                    continue
+                de(u, 16 * u, 128 * h + 128)
+                if u < 8 * h + 7: dup(h, u, 16 * u + 16, 128 * h + 128, "L4")
+                dup(h, u, 16 * u, 16 * u + 16, "LW", u == 8 * h + 7)
         vop(lambda v: v.tensor_scalar(T.pE[:, 0:256], T.pE[:, 0:256], 0.0, 8192.0, OP.is_ge, OP.mult), 256, pr=["pE"], pw=["pE"], name="nlq")
         tt(T.fz[:], T.ZQ[:], T.pE[:, 0:256], OP.max, 256, r=[W("ZQ")], w=[W("fz")], pr=["pE"], name="fz")
         for h in H:
             vop(lambda v, h=h: v.tensor_tensor_scan(T.FS[:, S(h)], T.NF[:], T.fz[:, S(h)], 0.0, OP.mult, OP.add), 128, r=[W("NF"), ("fz", 128 * h, 128 * h + 128)], w=[("FS", 128 * h, 128 * h + 128)], name="FS")
         tt(T.fl[:], T.FS[:, 15::16], T.DL[:], OP.min, 16, r=[W("FS"), W("DL")], w=[W("fl")], name="fl")
-        cpv(T.FZ[:], T.fl[:], 16, r=[W("fl")], w=[W("FZ")], name="FZ")
+        ts(T.FZ[:], T.fl[:], -1.0, OP.add, 16, r=[W("fl")], w=[W("FZ")], name="FZ")
         vop(lambda v: v.tensor_copy(T.O[:].indirect(T.FZ[:]), T.NC[:]), 256, r=[W("NC"), W("FZ")], w=[W("O")], two=3.0, name="scatter")
         G["wr"]["O"] = [y for y in G["wr"]["O"]]
         for h in H:
@@ -506,9 +539,10 @@ def build(core, T, topo, rank):
             cr = lambda n: (n, 96 * h, 96 * h + 96)
             tt(T.CLk[:, 96 * h:96 * h + 96], T.CLf[:, 96 * h:96 * h + 96], T.KP[:, t], OP.mult, 96, r=[cr("CLf"), W("KP%d" % t)], w=[cr("CLk")], name="CLk")
             tt(B("BDc", h)[:], B("nC", h)[:], T.PM[:, t], OP.mult, 128, r=[x("nC"), W("PM%d" % t)], w=[x("BDc")], name="BDc")
-            mm(C[:, :, 0:12], B("BDc", h)[:], T.U4[:], True, True, ck, 96, r=[x("BDc"), W("U4")], f32=True, name="CLp")
-            tt(T.CLf[:, 96 * h:96 * h + 96], T.CLk[:, 96 * h:96 * h + 96], C[:, :, 0:12], OP.add, 96, r=[cr("CLk")], w=[cr("CLf")], pr=[ck], name="CLf")
-            if not last: cpv(T.CLu[:, 96 * h:96 * h + 96], T.CLf[:, 96 * h:96 * h + 96], 96, r=[cr("CLf")], w=[cr("CLu")], name="CLu")
+            mm(C[:, :, 0:12], T.If[:], T.CLk[:, 96 * h:96 * h + 96], True, False, ck, 96, r=[cr("CLk"), W("If")], f32=True, name="CLp")
+            mm(C[:, :, 0:12], B("BDc", h)[:], T.U4[:], False, True, ck, 96, r=[x("BDc"), W("U4")], f32=True, name="CLp")
+            if not last: cpv(T.CLu[:, 96 * h:96 * h + 96], C[:, :, 0:12], 96, w=[cr("CLu")], pr=[ck], name="CLu")
+            act(T.CLf[:, 96 * h:96 * h + 96], C[:, :, 0:12], 96, w=[cr("CLf")], pr=[ck], name="CLf")
         if last: break
         for h in H:
             mm(T.pA1[:, :, 58], T.ONE[:], B("win", h)[:, 0::16], h == 0, h == 1, "pA1", 8, r=[W("win%d" % h), W("ONE")], name="ZC")

from concourse.bass import DstId, RemoteDMATransfer
from concourse.mybir import dt, AluOpType, AxisListType, ActivationFunctionType

V_, RO, NR = 3072, 4, 4
PAD = 256
OP = AluOpType
COPY = ActivationFunctionType.Copy
IDENT = ActivationFunctionType.Identity


def _decl():
    s = {}

    def sb(name, shape, dtype):
        s[name] = ("sbuf", shape, dtype)
    f, b, i, u = "float32", "bfloat16", "int32", "uint16"
    sb("O", [128, V_ + PAD], f); sb("OI", [128, V_], i); sb("XX", [128, 2 * V_], b); sb("CC", [128, V_], b)
    for d in (1, 2, 3): sb("WC%d" % d, [128, V_], b)
    sb("CI", [128, 192], i); sb("CF", [128, 192], f); sb("HL0", [128, 384], b)
    sb("TI", [128, 192], i); sb("TF", [128, 192], f); sb("CLf", [128, 192], f); sb("CLk", [128, 192], f); sb("CLu", [128, 192], u)
    for r in range(NR): sb("L0_%d" % r, [128, 384], b)
    sb("LU", [128, 12, 2, 8, 2], b); sb("SND", [128, 3, 2, 8, 2], b)
    for t in range(2): sb("VT%d" % t, [128, 4096], f)
    sb("VR", [128, 4, 256], f); sb("PM", [128, 4, 128], f); sb("KP", [128, 4, 96], f)
    sb("VC", [128, 16], f)
    for n in ("XK", "CG", "ST", "MN", "XM"): sb(n, [128, 2, 2048], b)
    sb("MX", [128, 2, 4, 8, 64], b); sb("E", [128, 2, 8, 8, 16], b); sb("PR", [128, 2, 15, 8, 16], b)
    for n in ("cS", "RM", "BR", "oh", "w", "brep", "BD", "cKv", "q2", "pz", "pc", "nC0", "nC", "BDc", "OC", "OE"): sb(n, [128, 2, 128], f)
    for n in ("nm", "XB", "SX", "wp", "win", "el", "oh2_"): sb(n, [128, 2, 128], b)
    sb("mS", [128, 2, 8, 24], b); sb("LM", [128, 256], u); sb("BZ", [128, 2, 128], f); sb("kS", [128, 2, 128], f); sb("HLz", [128, 2, 8, 16], b)
    sb("LA", [128, 256], u); sb("LB", [128, 16], u); sb("ZL", [128, 16], u); sb("FZ", [128, 16], u); sb("ZU", [128, 256], u)
    for n in ("aD", "ZQ", "ZS", "NC", "nlq", "fz", "FS", "XO", "QM"): sb(n, [128, 256], f)
    sb("fl", [128, 16], f); sb("DL", [128, 16], f); sb("DE", [128, 4096], b)
    for n in ("Ib", "Im", "Im16", "I256", "I16", "I3072", "BOb", "BN", "L4", "LW", "ONE", "K1", "K2"): sb(n, [128, 128], b)
    for n in ("If", "BOf", "NF"): sb(n, [128, 128], f)
    for n in ("DC", "C128", "oK"): sb(n, [128, 256], b)
    for n in ("VH", "VL"): sb(n, [128, 4, 256], b)
    for n in ("S1", "S16", "S32", "Sm16", "SHL"): sb(n, [128, 8], b)
    sb("U8", [128, 8], f); sb("U4", [128, 96], f)
    sb("ci", [128, 256], f); sb("cg", [128, 256], f); sb("cq", [128, 256], f)
    sb("pi", [128, 1], i); sb("ti", [128, 16], i); sb("tf", [128, 16], f); sb("wq", [128, 16], f)
    sb("zr", [128, 4], f); sb("zi", [128, 4], i); sb("Zc", [128, 1], f)
    for n in ("pA0", "pA1", "pB0", "pB1", "pC0", "pC1", "pD"): s[n] = ("psum", [128, 8, 64], f)
    s["pE"] = ("psum", [128, 512], f)
    return s


SCRATCH = _decl()
SEMAPHORES = ["cV", "cS", "cP", "cG", "loc"] + ["d%d" % k for k in range(52)] + ["ar%d_%d" % (t, r) for t in range(4) for r in range(NR)]
PS = ("pA0", "pA1", "pB0", "pB1", "pC0", "pC1", "pD", "pE")
D_OF = [1 + t % 3 for t in range(RO)]
CYC = 0.83e-3
WAKE = 0.09
GCY = 1.5
ASG = {"XK1": "S", "CG0": "S", "CG1": "S", "XM0": "S", "XM1": "S", "compose0": "S", "compose1": "S", "compose2": "S", "compose3": "S"}
NPC, NPM, NPS = 2, 2, 8
WT = {'ST': -10, 'SX': -5, 'zr': -10, 'key': 10, 'XB1': 10, 'RW': 20, 'BDc': -10, 'LM': -10, 'LA': 2, 'compose1': 10, 'RM': 2, 'pc': -10, 'pz': -5, 'ld sha': 10, 'el': -20, 'q2': 20, 'cL': 20, 'ZQ': -20, 'ext': -5, 'win': -2, 'oh2T': 10, 'CLu': -10, 'mS': 10, 'HLz': 2, 'oh2': 10, 'VT': -10, 'XM0': -2, 'csv': -2, 'flat': -2, 'CLk': 5, 'nk': 2, 'ZU': 10, 'Zc': -2, 'LMa': 20, 'CLf': -20, 'OC': 10, 'ld ctl': 5, 'nlq': 20, 'ld list': 20, 'send': 20, 'nC0': 10, 'hb': 2, 'bmv': 2, 'lo': 2, 'ld hol': 10, 'a1': 10, 'CF': -5, 'sendb': 5, 'zm': 20, 'fl': -2, 'OE': 20, 'DUP1': -5, 'FZ': -5, 'nC': 2, 'RM2': -20, 'sp': 10, 'scatter': 5, 'SXc': -10, 'WCu': -10, 'wp': 10, 'cKv': -2, 'XO': -2, 'compose3': 10, 'st yo': 5, 'hi': 5, 'O': 5}
MXS = ()
PRS = ()


def new_graph():
    return {"ops": [], "wr": {}, "rd": {}, "bw": {}, "br": {}}


def add(G, opts, fn, r=(), w=(), pr=(), pw=(), key=None, cnt=1, name=""):
    n = len(G["ops"])
    deps = {}

    def dep(j, raw):
        if j != n: deps[j] = deps.get(j, False) or raw
    for (bn, lo, hi) in r:
        for (a, b, j) in G["wr"].get(bn, []):
            if a < hi and lo < b: dep(j, True)
        G["rd"].setdefault(bn, []).append((lo, hi, n))
    for (bn, lo, hi) in w:
        for (a, b, j) in G["wr"].get(bn, []):
            if a < hi and lo < b: dep(j, False)
        for (a, b, j) in G["rd"].get(bn, []):
            if a < hi and lo < b: dep(j, False)
        G["wr"][bn] = [x for x in G["wr"].get(bn, []) if not (lo <= x[0] and x[1] <= hi)] + [(lo, hi, n)]
        G["rd"][bn] = [x for x in G["rd"].get(bn, []) if not (lo <= x[0] and x[1] <= hi)]
    engs = tuple(sorted(opts))
    for bn in pr:
        if bn in G["bw"]: dep(G["bw"][bn], True)
        for j in G["br"].get(bn, []):
            if G["ops"][j]["engs"] != engs or len(engs) > 1: dep(j, False)
        G["br"].setdefault(bn, []).append(n)
    for bn in pw:
        if bn in G["bw"]: dep(G["bw"][bn], False)
        for j in G["br"].get(bn, []): dep(j, False)
        G["bw"][bn] = n; G["br"][bn] = []
    G["ops"].append({"opts": opts, "engs": engs, "fn": fn, "deps": deps, "key": key, "cnt": cnt, "name": name})
    return n


def schedule(G, wake=WAKE, quant=0.08):
    ops = G["ops"]; n = len(ops)
    succ = [[] for _ in range(n)]; ind = [len(o["deps"]) for o in ops]
    for i, o in enumerate(ops):
        for j in o["deps"]: succ[j].append(i)
    prio = [0.0] * n
    for i in range(n - 1, -1, -1):
        d = min(x[1] for x in ops[i]["opts"].values())
        prio[i] = d + max([prio[s] + 0.5 * wake for s in succ[i]] or [0.0])
    prio = [p + WT.get(o["name"], 0.0) for p, o in zip(prio, ops)]
    free = {}; fin = [0.0] * n; eng = [None] * n; rdy = {}
    order = []; t_ready = [0.0] * n
    for i in range(n):
        if ind[i] == 0: rdy[i] = True
    while rdy:
        best = None
        for i in rdy:
            for e, c in ops[i]["opts"].items():
                st = free.get(e, 0.0)
                for j, raw in ops[i]["deps"].items():
                    x = fin[j] + (wake if eng[j] != e else (0.06 if raw else -1.0))
                    if x > st: st = x
                k = (int(st / quant), -prio[i], st)
                if best is None or k < best[0]: best = (k, i, e, st)
        _, i, e, st = best
        del rdy[i]
        c = ops[i]["opts"][e]
        free[e] = st + c[0]; fin[i] = st + c[1]; eng[i] = e; t_ready[i] = st
        order.append(i)
        for s in succ[i]:
            ind[s] -= 1
            if ind[s] == 0: rdy[s] = True
    return order, eng, fin, t_ready


def vc(n, two=1.0): return max(64.0, n * two) * CYC * 1.2 + 0.01
def sc(n): return max(64.0, n) * CYC * 1.2 + 0.03
def pc_(n, f32=False): return max(64.0, n) * CYC * 1.1 * (4.0 if f32 else 1.0) + 0.01


def build(core, T, topo, rank):
    G = new_graph()
    W = lambda n: (n, 0, 1 << 20)
    nd = [0]

    def vop(fn, n, r=(), w=(), pr=(), pw=(), two=1.0, name=""):
        c = vc(n, two)
        return add(G, {"V": (c, c)}, lambda Q, e: fn(Q["V"]), r, w, pr, pw, name=name)

    def tt(o, a, b, op, n, r=(), w=(), pr=(), name="", pw=(), two=None):
        vop(lambda v: v.tensor_tensor(o, a, b, op), n, r, w, pr, pw, two=two or (1.0 if pr else 2.0), name=name)

    def ts(o, a, s1, op0, n, r=(), w=(), pr=(), s2=None, op1=None, two=1.0, name=""):
        if op1 is None: vop(lambda v: v.tensor_scalar(o, a, s1, None, op0), n, r, w, pr, two=two, name=name)
        else: vop(lambda v: v.tensor_scalar(o, a, s1, s2, op0, op1), n, r, w, pr, two=two, name=name)

    def cpv(o, a, n, r=(), w=(), pr=(), name=""):
        vop(lambda v: v.tensor_copy(o, a), n, r, w, pr, name=name)

    def flex(o, a, n, r=(), w=(), pr=(), name="", cyc=1.0, only=None):
        opts = {"V": (vc(n, cyc), vc(n, cyc)), "S": (sc(n * cyc), sc(n * cyc))}
        only = only or ASG.get(name)
        if only: opts = {only: opts[only]}
        return add(G, opts, lambda Q, e: Q["V"].tensor_copy(o, a) if e == "V" else Q["S"].activation(o, a, COPY), r, w, pr, name=name)

    def act(o, a, n, func=COPY, bias=0.0, scale=1.0, r=(), w=(), pr=(), name="", pw=()):
        return add(G, {"S": (sc(n), sc(n))}, lambda Q, e: Q["S"].activation(o, a, func, bias=bias, scale=scale), r, w, pr, pw, name=name)

    def mm(o, l, rh, start, stop, bank, n, r=(), f32=False, name=""):
        c = pc_(n, f32)
        return add(G, {"P": (c, c)}, lambda Q, e: Q["P"].matmul(o, l, rh, start, stop), r, (), (), (bank,), name=name)

    def gop(fn, n, r=(), w=(), name=""):
        c = 0.14 + 2 * n * CYC * 1.2
        return add(G, {"G": (c, c)}, lambda Q, e: fn(Q["G"]), r, w, name=name)

    def dma(o, a, kb, r=(), w=(), q="Y", name=""):
        k = nd[0]; nd[0] += 1
        return add(G, {q: (0.1, 2.0 + kb / 200.0)}, lambda Q, e: (Q["Y"] if e == "Y" else Q["S"]).dma_start(o, a).then_inc(T.sem["d%d" % k], 16), r, w, key="d%d" % k, cnt=16, name=name)

    def send(dsts, src_ap, land, sem, r, kb, name):
        m = 255
        ne = len(topo.engines(core, dsts[0]))
        for x in dsts: assert topo.may_write(core, x) and topo.mask(core, x) == topo.mask(core, dsts[0])

        def fn(Q, e):
            if len(dsts) == 1:
                rid, pid = topo.addr(dsts[0])[:2]
                Q["G"].remote_dma(out_ap=land, in_ap=src_ap, remote_sem=T.sem[sem], local_sem=T.sem.loc, pid=pid, routing_id=rid, dma_engine_mask=topo.mask(core, dsts[0]))
            else:
                ids = [DstId(rid=topo.addr(x)[0], pnc=topo.addr(x)[1]) for x in dsts]
                Q["G"].remote_dma_fused([RemoteDMATransfer(dst_ids=ids, dma_engine_mask=topo.mask(core, dsts[0]), remote_sem=T.sem[sem], srcs=[src_ap], dsts=[land for x in dsts])], local_sem=T.sem.loc)
        return add(G, {"G": (1.0, 1.0)}, fn, r, (), key="loc", cnt=ne, name=name)

    def arrive(src_rank, t, after, kb):
        nm = "L%d_%d" % (t, src_rank)
        i = add(G, {"N%d_%d" % (t, src_rank): (0.0, 2.5 + kb / 40.0)}, None, (), (W(nm),), key="ar%d_%d" % (t, src_rank), cnt=len(topo.engines(T.cores[src_rank], core)), name="arrive")
        G["ops"][i]["deps"][after] = True

    H = (0, 1)

    def ext(X, bank):
        opts = {"V": (vc(64), vc(64)), "S": (sc(64), sc(64))}
        if "ext" in ASG: opts = {ASG["ext"]: opts[ASG["ext"]]}
        add(G, opts, lambda Q, e: Q["V"].tensor_copy(X[:, :, 16:24], X[:, :, 0:8]) if e == "V" else Q["S"].activation(X[:, :, 16:24], X[:, :, 0:8], COPY), (), (), (bank,), (bank,), name="ext")

    def P(n, h): return T["p" + n + str(h)]
    def B(n, h): return T[n][:, h]
    def LU(t, r): return T.LU[:, 4 * (t - 1) + r]

    dma(T.CI[:], T.ctl[:], 98, w=[W("CI")], name="ld ctl")
    for c in range(4):
        dma(T.OI[:, 768 * c:768 * c + 768], T.hol[:, 768 * c:768 * c + 768], 393, w=[("OI", 768 * c, 768 * c + 768)], q="Y", name="ld hol")
    for e in range(2):
        for b in range(6):
            dma(T.TI[:, 32 * b + 16 * e:32 * b + 16 * e + 16], T.ctl[e::2, 512 * b:512 * b + 512], 8, w=[("TI", 32 * b + 16 * e, 32 * b + 16 * e + 16)], q="S", name="ld list")
    for c in range(2):
        dma(T.XX[:, 1536 * c:1536 * c + 1536], T.sha[:, 1536 * c:1536 * c + 1536], 393, w=[("XX", 1536 * c, 1536 * c + 1536)], q="S", name="ld sha")
    cpv(T.CF[:], T.CI[:], 192, r=[W("CI")], w=[W("CF")], name="CF")
    cpv(T.HL0[:, 0:192], T.CF[:], 192, r=[W("CF")], w=[("HL0", 0, 192)])
    tt(T.HL0[:, 192:384], T.CF[:], T.HL0[:, 0:192], OP.subtract, 192, r=[W("CF"), ("HL0", 0, 192)], w=[("HL0", 192, 384)])
    me = T.cores[rank]
    first = T.cores[(rank - D_OF[0]) % NR]
    rest = [T.cores[(rank - d) % NR] for d in (1, 2, 3) if (rank - d) % NR != (rank - D_OF[0]) % NR]
    lands = "L0_%d" % rank
    s1 = send([first], T.HL0[:], T[lands][:], "ar0_%d" % rank, [W("HL0")], 98, "send0")
    s2 = send(rest, T.HL0[:], T[lands][:], "ar0_%d" % rank, [W("HL0")], 196, "send0b")
    gop(lambda g: g.iota(T.pi[:], [[1, 1]], 0, 1), 1, w=[W("pi")])
    gop(lambda g: g.iota(T.ci[:], [[1, 256]], 0, 0, allow_small_or_imprecise_dtypes=True), 256, w=[W("ci")])
    gop(lambda g: g.iota(T.cg[:], [[1, 16], [0, 16]], 0, 0, allow_small_or_imprecise_dtypes=True), 256, w=[W("cg")])
    gop(lambda g: g.iota(T.cq[:], [[0, 16], [1, 16]], 0, 0, allow_small_or_imprecise_dtypes=True), 256, w=[W("cq")])
    gop(lambda g: g.iota(T.DL[:], [[16, 16]], V_, 0, allow_small_or_imprecise_dtypes=True), 16, w=[W("DL")])
    for t in range(RO):
        gop(lambda g, t=t: g.iota(T.VR[:, t], [[12, 256]], t, 0, allow_small_or_imprecise_dtypes=True), 256, w=[W("VR%d" % t)])

    def vt(t):
        for c in range(4):
            i = gop(lambda g, c=c: g.iota(T["VT%d" % (t % 2)][:, 1024 * c:1024 * c + 1024], [[12, 64], [0, 16]], t + 768 * c, 0, allow_small_or_imprecise_dtypes=True), 1024, w=[("VT%d" % (t % 2), 1024 * c, 1024 * c + 1024)], name="VT")
            G["ops"][i]["deps"][s2] = False
    vt(0)
    vt(1)
    for t in range(RO):
        gop(lambda g, t=t: g.iota(T.VH[:, t], [[48, 64], [0, 4]], 0, 0, allow_small_or_imprecise_dtypes=True), 256, w=[W("VH%d" % t)])
        gop(lambda g, t=t: g.iota(T.VL[:, t], [[0, 64], [12, 4]], t, 0, allow_small_or_imprecise_dtypes=True), 256, w=[W("VL%d" % t)])
    vop(lambda v: v.memset(T.WC1[:], 0.0), V_, w=[W("WC1")], two=0.5)
    for d in (2, 3):
        i = gop(lambda g, d=d: g.iota(T["WC%d" % d][:], [[0, V_]], 0, 0, allow_small_or_imprecise_dtypes=True), V_, w=[W("WC%d" % d)])
        G["ops"][i]["deps"][s2] = False
    for d in (1, 2, 3):
        s = (rank + d) % NR
        arrive(s, 0, s1 if d == D_OF[0] else s2, 98 if d == D_OF[0] else 196)
        for x in (0, 1):
            dma(T["WC%d" % d][x:128:16, :], T["L0_%d" % s][:, 192 * x:192 * x + 192], 49, r=[W("L0_%d" % s)], w=[W("WC%d" % d)] if x == 0 else [("WC%d" % d, 0, 1 << 19)], name="flat")
            if x == 0: G["wr"]["WC%d" % d] = [y for y in G["wr"]["WC%d" % d]]
    def sh(o, k): ts(T.ti[:, o:o + 1], T.pi[:], k, OP.arith_shift_right, 1, r=[W("pi")], w=[("ti", o, o + 1)])
    def an(o, src, k, rr): ts(T.ti[:, o:o + 1], src, k, OP.bitwise_and, 1, r=rr, w=[("ti", o, o + 1)])
    sh(1, 4); an(2, T.pi[:], 15, [W("pi")])
    cpv(T.ti[:, 0:1], T.pi[:], 1, r=[W("pi")], w=[("ti", 0, 1)])
    an(8, T.pi[:], 3, [W("pi")])
    ts(T.ti[:, 9:10], T.ti[:, 8:9], 12, OP.mult, 1, r=[("ti", 8, 9)], w=[("ti", 9, 10)])
    for t in range(RO):
        ts(T.ti[:, 10 + t:11 + t], T.ti[:, 9:10], t, OP.add, 1, r=[("ti", 9, 10)], w=[("ti", 10 + t, 11 + t)])
        an(3 + t, T.ti[:, 10 + t:11 + t], 15, [("ti", 10 + t, 11 + t)])
    ts(T.ti[:, 14:15], T.pi[:], 12, OP.mult, 1, r=[W("pi")], w=[("ti", 14, 15)])
    ts(T.ti[:, 7:8], T.ti[:, 14:15], 4, OP.arith_shift_right, 1, r=[("ti", 14, 15)], w=[("ti", 7, 8)])
    ts(T.ti[:, 15:16], T.ti[:, 1:2], 8, OP.add, 1, r=[("ti", 1, 2)], w=[("ti", 15, 16)])
    cpv(T.tf[:], T.ti[:], 16, r=[W("ti")], w=[W("tf")])
    F = lambda k: T.tf[:, k:k + 1]
    tfr = [W("tf")]
    for h in H:
        for t in range(RO):
            k = 2 * t + h
            ts(T.VC[:, k:k + 1], F(0), 12.0, OP.mult, 1, r=tfr, w=[("VC", k, k + 1)], s2=float(12 * 128 * h + t), op1=OP.add)
            ts(T.VC[:, 8 + k:9 + k], F(0), -12.0, OP.mult, 1, r=tfr, w=[("VC", 8 + k, 9 + k)], s2=float(-12 * 128 * h - t), op1=OP.add)
    ts(T.DL[:], T.DL[:], F(2), OP.add, 16, r=tfr + [W("DL")], w=[W("DL")])
    ci = T.ci[:, 0:128]; rc = tfr + [W("ci")]; rq = tfr + [W("cq")]; rg = tfr + [W("cg")]
    ts(T.If[:], ci, F(0), OP.is_equal, 128, r=rc, w=[W("If")])
    ts(T.BOf[:], T.cg[:, 0:128], F(1), OP.is_equal, 128, r=rg, w=[W("BOf")])
    for src, nmx, s in (("If", "Ib", 1.0), ("If", "Im", -1.0), ("If", "Im16", -16.0), ("If", "I16", 16.0), ("If", "I3072", 3072.0), ("BOf", "BOb", 1.0), ("BOf", "L4", 4.0), ("BOf", "BN", -128.0)):
        act(T[nmx][:], T[src][:], 128, COPY, scale=s, r=[W(src)], w=[W(nmx)])
    ts(T.QM[:], T.cq[:], F(2), OP.is_equal, 256, r=rq, w=[W("QM")])
    ts(T.NF[:], T.cq[:, 0:128], 0.0, OP.not_equal, 128, r=[W("cq")], w=[W("NF")])
    for nmx, s in (("S1", 1.0), ("S16", 16.0), ("S32", 32.0)):
        ts(T[nmx][:], T.ci[:, 0:8], F(1), OP.is_equal, 8, r=rc, w=[W(nmx)], s2=s, op1=OP.mult)
    ts(T.wq[:, 0:1], F(2), 1.0, OP.is_le, 1, r=tfr, w=[("wq", 0, 1)])
    ts(T.SHL[:], T.ci[:, 0:8], F(1), OP.is_equal, 8, r=rc + [("wq", 0, 1)], w=[W("SHL")], s2=T.wq[:, 0:1], op1=OP.mult)
    ts(T.U8[:], T.ci[:, 0:8], F(1), OP.is_equal, 8, r=rc, w=[W("U8")])
    ts(T.U4[:], T.ci[:, 0:96], F(7), OP.is_equal, 96, r=rc, w=[W("U4")])
    for t in range(RO): ts(T.PM[:, t], T.cq[:, 0:128], F(3 + t), OP.is_equal, 128, r=rq, w=[W("PM%d" % t)])
    ts(T.K1[:], T.cq[:, 0:128], -1.0, OP.mult, 128, r=[W("cq")], w=[W("K1")], s2=15.0, op1=OP.add)
    ts(T.K2[:], T.cq[:, 0:128], -1.0, OP.mult, 128, r=[W("cq")], w=[W("K2")], s2=31.0, op1=OP.add)
    vop(lambda v: v.memset(T.ONE[:], 1.0), 128, w=[W("ONE")])
    for q in range(16): vop(lambda v, q=q: v.memset(T.fz[:, q::16], 2.0 ** -q), 16, w=[W("fz")])
    tt(T.FS[:], T.fz[:], T.QM[:], OP.mult, 256, r=[W("fz"), W("QM")], w=[W("FS")])
    vop(lambda v: v.tensor_reduce(T.wq[:, 1:2], T.FS[:, 0:16], AxisListType.X, OP.add), 16, r=[W("FS")], w=[("wq", 1, 2)])
    ts(T.LW[:], T.BOf[:], T.wq[:, 1:2], OP.mult, 128, r=[W("BOf"), ("wq", 1, 2)], w=[W("LW")])
    ts(T.nlq[:], T.QM[:], 1024.0, OP.mult, 256, r=[W("QM")], w=[W("nlq")], s2=-1024.0, op1=OP.add)
    act(T.C128[:], T.QM[:], 256, COPY, scale=128.0, r=[W("QM")], w=[W("C128")])
    ts(T.DL[:], T.DL[:], 1.0, OP.add, 16, r=[W("DL")], w=[W("DL")])
    ts(T.ZQ[:], T.FS[:], -2.0, OP.mult, 256, r=[W("FS")], w=[W("ZQ")])
    tt(T.DC[:], T.nlq[:], T.ZQ[:], OP.add, 256, r=[W("nlq"), W("ZQ")], w=[W("DC")])
    vop(lambda v: v.memset(T.O[:, V_:V_ + PAD], 0.0), PAD, w=[("O", V_, V_ + PAD)])
    for h in H:
        vop(lambda v, h=h: v.memset(B("BZ", h)[:], 0.0), 128, w=[W("BZ%d" % h)])
        vop(lambda v, h=h: v.memset(B("HLz", h)[:], 0.0), 128, w=[W("HLz%d" % h)])
    vop(lambda v: v.memset(T.Zc[:], 9.0), 1, w=[W("Zc")])
    for t in range(RO):
        mm(T.pE[:, 0:96], T.PM[:, t], T.U4[:], True, True, "pE", 96, r=[W("PM%d" % t), W("U4")], f32=True)
        ts(T.KP[:, t], T.pE[:, 0:96], -1.0, OP.mult, 96, w=[W("KP%d" % t)], pr=["pE"], s2=1.0, op1=OP.add)
    cpv(T.TF[:], T.TI[:], 192, r=[W("TI")], w=[W("TF")])
    vop(lambda v: v.transpose(T.CLf[:], T.TF[:]), 192, r=[W("TF")], w=[W("CLf")])
    cpv(T.CLu[:], T.CLf[:], 192, r=[W("CLf")], w=[W("CLu")])
    for c in range(4):
        cpv(T.O[:, 768 * c:768 * c + 768], T.OI[:, 768 * c:768 * c + 768], 768, r=[("OI", 768 * c, 768 * c + 768)], w=[("O", 768 * c, 768 * c + 768)], name="O f32")
    for c in range(2):
        a, z = 1536 * c, 1536 * c + 1536
        add(G, {"V": (vc(1536, 0.5), vc(1536, 0.5)), "S": (sc(1536), sc(1536))},
            lambda Q, e, a=a, z=z: Q["V"].tensor_scalar(T.XX[:, V_ + a:V_ + z], T.XX[:, a:z], -1.0, None, OP.mult) if e == "V" else Q["S"].activation(T.XX[:, V_ + a:V_ + z], T.XX[:, a:z], COPY, scale=-1.0),
            [("XX", a, z)], [("XX", V_ + a, V_ + z)], name="-X")

    for t in range(RO):
        d = D_OF[t]; last = t == RO - 1
        wc = "WC%d" % d
        VT, VR = T["VT%d" % (t % 2)], T.VR[:, t]
        XR = [("XX", 0, V_)]
        hs = lambda h: slice(1536 * h + t, 1536 * h + 1536, 12)
        oreg = lambda h: ("O", 1536 * h, 1536 * h + 1536)
        S = lambda h: slice(128 * h, 128 * h + 128)
        for h in H:
            src = T.OI if t == 0 else T.O
            cpv(T.LA[:, S(h)], src[:, hs(h)], 128, r=[("OI" if t == 0 else "O", 1536 * h, 1536 * h + 1536)], w=[("LA", 128 * h, 128 * h + 128)], name="LA")
        for c in range(4):
            flex(T.CC[:, 768 * c:768 * c + 768], T[wc][:].indirect(T.CLu[:, 48 * c:48 * c + 48]), 768, r=[W(wc), W("CLu")], w=[("CC", 768 * c, 768 * c + 768)], cyc=GCY, name="compose%d" % c)
        la = lambda h: ("LA", 128 * h, 128 * h + 128)
        pieces = lambda n: [(2048 // n * p, 2048 // n * (p + 1), 128 // n * p, 128 // n * (p + 1)) for p in range(n)]
        for h in H:
            for a, z, c, e in pieces(NPC): flex(B("XK", h)[:, a:z], T.XX[:, 0:V_].indirect(T.LA[:, 128 * h + c:128 * h + e]), z - a, r=XR + [la(h)], w=[("XK%d" % h, a, z)], cyc=GCY, name="XK%d" % h)
        for h in H:
            for a, z, c, e in pieces(NPC): flex(B("CG", h)[:, a:z], T.CC[:].indirect(T.LA[:, 128 * h + c:128 * h + e]), z - a, r=[W("CC"), la(h)], w=[("CG%d" % h, a, z)], cyc=GCY, name="CG%d" % h)
        for h in H:
            for a, z, c, e in pieces(NPS):
                vop(lambda v, h=h, VT=VT, a=a, z=z, c=c, e=e: v.tensor_tensor(B("ST", h)[:, a:z], T.O[:, 0:V_].indirect(T.LA[:, 128 * h + c:128 * h + e]), VT[:, 2048 * h + a:2048 * h + z], OP.is_equal), z - a,
                    r=[("O", 0, V_), la(h), ("VT%d" % (t % 2), 2048 * h + a, 2048 * h + z)], w=[("ST%d" % h, a, z)], two=GCY, name="ST")
        if t + 2 < RO: vt(t + 2)
        for h in H:
            mm(P("C", h)[:, :, 0:16], T.Ib[:], T.XX[:, hs(h)], True, True, "pC%d" % h, 128, r=XR + [W("Ib")])
        for h in H:
            A = P("A", h); bk = "pA%d" % h
            for k in range(16):
                mm(A[:, :, k], B("CG", h)[:, k::16], T.SHL[:], True, True, bk, 8, r=[W("CG%d" % h), W("SHL")], name="cL")
            ext(A, bk)
            flex(B("cS", h)[:], A[:, :, 0:16], 128, w=[W("cS%d" % h)], pr=[bk], name="cS")
            for s in range(1, 9):
                tt(B("E", h)[:, s - 1], B("cS", h)[:], A[:, :, s:s + 16], OP.not_equal if h in PRS else OP.is_equal, 128, r=[W("cS%d" % h)], w=[("E%d" % h, s - 1, s)], pr=[bk], name="E")
        for h in H:
            if h in MXS: continue
            for k in range(16):
                mm(T.pE[:, 128 * h + k:128 * h + 128:16], B("XK", h)[:, k::16], T.S1[:], True, True, "pE", 8, r=[W("XK%d" % h), W("S1")], name="SX")
            act(B("SX", h)[:], T.pE[:, S(h)], 128, w=[W("SX%d" % h)], pr=["pE"], name="SXc")
        for h in H:
            Bk = P("B", h); bk = "pB%d" % h
            for k in range(16):
                tt(B("MN", h)[:, S(k)], B("XK", h)[:, k::16], P("C", h)[:, :, 0:16], OP.min, 128, r=[W("XK%d" % h)], w=[("MN%d" % h, 128 * k, 128 * k + 128)], pr=["pC%d" % h], name="MN")
            for k in range(16):
                mm(Bk[:, :, k], B("MN", h)[:, S(k)], T.S1[:], True, True, bk, 8, r=[("MN%d" % h, 128 * k, 128 * k + 128), W("S1")], name="mL")
            ext(Bk, bk)
            mS = B("mS", h)
            nx = 24 if h in PRS else 16
            flex(mS[:, :, 0:nx], Bk[:, :, 0:nx], 8 * nx, w=[W("mS%d" % h)], pr=[bk], name="mS")
            PRh, Eh = B("PR", h), B("E", h)
            for c in range(4 if h in PRS else 0):
                bn = "pE" if c % 2 else bk
                n = min(4, 15 - 4 * c)
                for jj in range(n):
                    j = 4 * c + jj
                    s = j + 1 if j < 8 else j - 7
                    o = T.pE[:, S(jj)] if c % 2 else Bk[:, 2 * jj:2 * jj + 2, :]
                    mm(o, T.Ib[:], mS[:, :, s:s + 16] if j < 8 else mS[:, :, 0:16], True, False, bn, 128, r=[W("mS%d" % h), W("Ib")], name="PRm")
                    mm(o, T.I256[:], Eh[:, s - 1], False, True, bn, 128, r=[("E%d" % h, s - 1, s), W("I256")], name="PRm")
                act(PRh[:, 4 * c:4 * c + n], T.pE[:, 0:128 * n] if c % 2 else Bk[:, 0:2 * n, :], 128 * n, ActivationFunctionType.Relu, w=[("PR%d" % h, 4 * c, 4 * c + n)], pr=[bn], name="PRa")
            for s in range(1, 9 if h not in PRS else 0):
                tt(PRh[:, s - 1], Eh[:, s - 1], Bk[:, :, s:s + 16], OP.mult, 128, r=[("E%d" % h, s - 1, s)], w=[("PR%d" % h, s - 1, s)], pr=[bk], name="PR")
            for s in range(1, 8 if h not in PRS else 0):
                tt(PRh[:, 7 + s], Eh[:, s - 1], Bk[:, :, 0:16], OP.mult, 128, r=[("E%d" % h, s - 1, s)], w=[("PR%d" % h, 7 + s, 8 + s)], pr=[bk], name="PR")
            C = P("C", h); ck = "pC%d" % h
            mm(C[:, :, 16:32], T.Ib[:], T.K1[:], True, False, ck, 128, r=[W("Ib"), W("K1")], name="key")
            mm(C[:, :, 16:32], T.I16[:], mS[:, :, 0:16], False, False, ck, 128, r=[W("I16"), W("mS%d" % h)], name="key")
            for s in range(1, 9):
                mm(C[:, :, 16:32], T.I16[:], PRh[:, s - 1], False, False, ck, 128, r=[("PR%d" % h, s - 1, s)], name="key")
            for s in range(1, 8):
                mm(C[:, :, 16 + s:32], T.I16[:], PRh[:, 7 + s, :, 0:16 - s], False, False, ck, 128 - 8 * s, r=[("PR%d" % h, 7 + s, 8 + s)], name="key")
                mm(C[:, :, 16:16 + s], T.I16[:], PRh[:, 7 + s, :, 16 - s:16], False, s == 7, ck, 8 * s, r=[("PR%d" % h, 7 + s, 8 + s)], name="key")

        def spread(h, src, sreg, fin, freg, floor=None, bank=None):
            bz = B("BZ", h); zr = [W("BZ%d" % h)]
            if floor is None: cpv(bz[:, 0::16], src[:, 15::16], 8, r=[sreg], w=zr, name="sp")
            else: ts(bz[:, 0::16], src[:, 15::16], floor, OP.max, 8, r=[sreg], w=zr, name="sp")
            vop(lambda v: v.tensor_tensor_scan(fin, T.NF[:], bz[:], 0.0, OP.mult, OP.add), 128, r=zr + [W("NF")], w=[freg] if freg else [], pw=[bank] if bank else [], name="sp")

        for h in H:
            A, C = P("A", h), P("C", h); ak, ck = "pA%d" % h, "pC%d" % h
            x = lambda n: W(n + str(h))
            flex(B("kS", h)[:], C[:, :, 16:32], 128, w=[x("kS")], pr=[ck], name="kS")
            vop(lambda v, h=h: v.tensor_tensor_scan(B("RM", h)[:], T.NF[:], B("kS", h)[:], 0.0, OP.mult, OP.max), 128, r=[W("NF"), x("kS")], w=[x("RM")], name="RM")
            spread(h, B("RM", h), x("RM"), B("BR", h), x("BR"))
            tt(B("oh", h)[:], B("BR", h)[:], C[:, :, 16:32], OP.is_equal, 128, r=[x("BR")], w=[x("oh")], pr=[ck], name="oh")
            tt(B("w", h)[:], B("oh", h)[:], A[:, :, 0:16], OP.mult, 128, r=[x("oh")], w=[x("w")], pr=[ak], name="w")
            vop(lambda v, h=h: v.tensor_tensor_scan(B("RM", h)[:], T.NF[:], B("w", h)[:], 0.0, OP.mult, OP.add), 128, r=[W("NF"), x("w")], w=[x("RM")], name="RW")
            spread(h, B("RM", h), x("RM"), B("brep", h), x("brep"))
            tt(B("nm", h)[:], B("brep", h)[:], A[:, :, 0:16], OP.not_equal, 128, r=[x("brep")], w=[x("nm")], pr=[ak], name="nm")
            mm(C[:, :, 48:64], T.If[:], T.O[:, hs(h)], True, False, ck, 128, r=[oreg(h), W("If")], f32=True, name="LMa")
            mm(C[:, :, 48:64], B("nm", h)[:], T.I3072[:], False, True, ck, 128, r=[x("nm"), W("I3072")], name="LMn")
            cpv(T.LM[:, S(h)], C[:, :, 48:64], 128, w=[x("LM")], pr=[ck], name="LM")
            for a, z, c, e in pieces(NPM): flex(B("XM", h)[:, a:z], T.XX[:].indirect(T.LM[:, 128 * h + c:128 * h + e]), z - a, r=[W("XX"), x("LM")], w=[("XM%d" % h, a, z)], cyc=GCY, name="XM%d" % h)
            tt(B("BD", h)[:], B("brep", h)[:], T.QM[:, 0:128], OP.mult, 128, r=[x("brep"), W("QM")], w=[x("BD")], name="BD")
            mm(A[:, :, 56], B("BD", h)[:], T.U8[:], True, True, ak, 8, r=[x("BD"), W("U8")], f32=True, name="LBp")
            cpv(T.LB[:, 8 * h:8 * h + 8], A[:, :, 56], 8, w=[("LB", 8 * h, 8 * h + 8)], pr=[ak], name="LB")
            flex(B("XB", h)[:], T.XX[:, 0:V_].indirect(T.LB[:, 8 * h:8 * h + 8]), 128, r=XR + [("LB", 8 * h, 8 * h + 8)], w=[x("XB")], cyc=GCY, name="XB%d" % h)
            if h not in MXS: mm(C[:, :, 32:48], T.Ib[:], B("XB", h)[:], True, True, ck, 128, r=[x("XB")], name="XBp")
        for h in H:
            A, C, Bk = P("A", h), P("C", h), P("B", h); ak, ck, bk = "pA%d" % h, "pC%d" % h, "pB%d" % h
            x = lambda n: W(n + str(h))
            mm(A[:, :, 40:56], B("cS", h)[:], T.If[:], True, False, ak, 128, r=[x("cS"), W("If")], f32=True, name="cK")
            mm(A[:, :, 40:56], T.Im[:], T.VH[:, t, S(h)], False, False, ak, 128, r=[W("Im"), W("VH%d" % t)], name="cK")
            mm(A[:, :, 40:56], T.Im[:], T.VL[:, t, S(h)], False, True, ak, 128, r=[W("Im"), W("VL%d" % t)], name="cK")
            act(B("cKv", h)[:], A[:, :, 40:56], 128, w=[x("cKv")], pr=[ak], name="cKv")
            MX = B("MX", h)
            if h in MXS:
                for c in range(4):
                    bn = ck if c % 2 else "pE"
                    for kk in range(4):
                        o = C[:, :, 16 * kk:16 * kk + 16] if c % 2 else T.pE[:, S(kk)]
                        mm(o, T.Ib[:], B("XK", h)[:, 4 * c + kk::16], True, False, bn, 128, r=[x("XK")], name="DF")
                        mm(o, T.Im[:], B("XB", h)[:], False, True, bn, 128, r=[x("XB")], name="DF")
                    act(MX[:, c], C[:] if c % 2 else T.pE[:], 512, ActivationFunctionType.Abs, w=[("MX%d" % h, 4 * c, 4 * c + 4)], pr=[bn], name="MXa")
            else:
                for k in range(16):
                    tt(MX[:, k // 4, 2 * (k % 4):2 * (k % 4) + 2], B("XK", h)[:, k::16], C[:, :, 32:48], OP.max, 128, r=[x("XK")], w=[("MX%d" % h, k, k + 1)], pr=[ck], name="MX")
            mm(A[:, :, 24:40], T.Ib[:], T.K2[:], True, False, ak, 128, r=[W("Ib"), W("K2")], name="FL")
            if h not in MXS: mm(A[:, :, 24:40], T.Im16[:], B("SX", h)[:], False, False, ak, 128, r=[W("Im16"), x("SX")], name="FL")
            for k in range(16):
                c, kk = divmod(k, 4)
                mr = [("MX%d" % h, k, k + 1)]
                if h in MXS:
                    l = MX[:, c, :, 16 * kk:16 * kk + 16] if c % 2 else MX[:, c, 2 * kk:2 * kk + 2]
                    mm(A[:, :, 24 + k], l, T.S16[:], False, k == 15, ak, 8, r=mr + [W("S16")], name="FL")
                else:
                    mm(A[:, :, 24 + k], MX[:, c, 2 * kk:2 * kk + 2], T.S32[:], False, k == 15, ak, 8, r=mr + [W("S32")], name="FL")
            for k in range(16):
                mm(Bk[:, :, 24 + k], B("ST", h)[:, k::16], T.S1[:], True, True, bk, 8, r=[x("ST"), W("S1")], name="SL")
            tt(B("el", h)[:], B("nm", h)[:], Bk[:, :, 24:40], OP.min, 128, r=[x("nm")], w=[x("el")], pr=[bk], name="el")
            tt(Bk[:, :, 0:16], B("el", h)[:], A[:, :, 24:40], OP.mult, 128, r=[x("el")], pr=[ak], pw=[bk], name="q1")
            mm(C[:, :, 0:16], B("brep", h)[:], T.If[:], True, True, ck, 128, r=[x("brep"), W("If")], f32=True, name="bR")
            act(T.aD[:, S(h)], T.O[:, hs(h)], 128, COPY, bias=1.0, r=[oreg(h)], w=[("aD", 128 * h, 128 * h + 128)], name="a1")
            act(C[:, :, 16:32], B("brep", h)[:], 128, IDENT, bias=T.VC[:, 8 + 2 * t + h:9 + 2 * t + h], r=[x("brep"), W("VC")], pw=[ck], name="bmv")
        for h in H:
            Bk = P("B", h); bk = "pB%d" % h
            x = lambda n: W(n + str(h))
            ws = T.pD[:, :, 16 * h:16 * h + 16]
            for p in range(NPM):
                ln = 8 // NPM
                for k in range(16):
                    mm(T.pD[:, ln * p:ln * p + ln, 16 * h:16 * h + 16], T.Ib[:], B("XM", h)[:, 2048 // NPM * p + k:2048 // NPM * (p + 1):16], k == 0, k == 15, "pD", 128 // NPM, r=[("XM%d" % h, 2048 // NPM * p, 2048 // NPM * (p + 1))], name="WS")
            ts(B("wp", h)[:], ws, 0.0, OP.is_gt, 128, w=[x("wp")], pr=["pD"], name="wp")
            wn = T.pD[:, :, 32 + 16 * h:48 + 16 * h]
            mm(wn, B("wp", h)[:], T.BOb[:], True, True, "pD", 128, r=[x("wp"), W("BOb")], name="WN")
            ts(B("win", h)[:], wn, T.Zc[:, 0:1], OP.is_ge, 128, r=[W("Zc")], w=[x("win")], pr=["pD"], name="win")
            tt(B("nC0", h)[:], B("win", h)[:], P("C", h)[:, :, 16:32], OP.mult, 128, r=[x("win")], w=[x("nC0")], pr=["pC%d" % h], name="nC0")
            ts(B("nC", h)[:], B("nC0", h)[:], T.VC[:, 2 * t + h:2 * t + h + 1], OP.add, 128, r=[x("nC0"), W("VC")], w=[x("nC")], name="nC")
            if not last:
                SN = T.SND[:, t]; sr = lambda o: ("SND%d" % t, 2 * h + o, 2 * h + o + 1)
                cpv(SN[:, h, :, 0], B("nC", h)[:, 0::16], 8, r=[x("nC")], w=[sr(0)], name="hi")
                tt(SN[:, h, :, 1], B("nC", h)[:, 0::16], SN[:, h, :, 0], OP.subtract, 8, r=[x("nC"), sr(0)], w=[sr(1)], name="lo")
        if not last:
            ds = [D_OF[u] for u in range(t + 1, RO)]
            land = LU(t + 1, rank); sem = "ar%d_%d" % (t + 1, rank)
            sa = send([T.cores[(rank - ds[0]) % NR]], T.SND[:, t], land, sem, [W("SND%d" % t)], 8, "send")
            sb_ = send([T.cores[(rank - q) % NR] for q in ds[1:]], T.SND[:, t], land, sem, [W("SND%d" % t)], 8, "sendb") if len(ds) > 1 else None
        for h in H:
            A, Bk, C = P("A", h), P("B", h), P("C", h); ak, bk, ck = "pA%d" % h, "pB%d" % h, "pC%d" % h
            x = lambda n: W(n + str(h))
            tt(B("q2", h)[:], B("win", h)[:], Bk[:, :, 0:16], OP.mult, 128, r=[x("win")], w=[x("q2")], pr=[bk], name="q2")
            vop(lambda v, h=h: v.tensor_tensor_scan(B("RM", h)[:], T.NF[:], B("q2", h)[:], 0.0, OP.mult, OP.max), 128, r=[W("NF"), x("q2")], w=[x("RM")], name="RM2")
            best = T.pE[:, 256 + 128 * h:384 + 128 * h]
            spread(h, B("RM", h), x("RM"), best, None, floor=0.5, bank="pE")
            tt(B("oh2_", h)[:], B("q2", h)[:], best, OP.is_equal, 128, r=[x("q2")], w=[x("oh2_")], pr=["pE"], name="oh2")
            mm(Bk[:, :, 0:16], B("oh2_", h)[:], T.Ib[:], True, True, bk, 128, r=[x("oh2_")], name="oh2T")
            tt(B("pz", h)[:], T.aD[:, S(h)], Bk[:, :, 0:16], OP.mult, 128, r=[("aD", 128 * h, 128 * h + 128)], w=[x("pz")], pr=[bk], name="pz")
            tt(B("pc", h)[:], B("cKv", h)[:], Bk[:, :, 0:16], OP.mult, 128, r=[x("cKv")], w=[x("pc")], pr=[bk], name="pc")
            hr = lambda n: (n, 128 * h, 128 * h + 128)
            act(T.oK[:, S(h)], Bk[:, :, 0:16], 128, w=[hr("oK")], pr=[bk], name="oK")
            act(C[:, :, 32:48], Bk[:, :, 0:16], 128, COPY, bias=1.0, scale=-1.0, pr=[bk], pw=[ck], name="nk")
            zm = T.pD[:, :, 32 + 16 * h:48 + 16 * h]
            mm(zm, T.BOf[:], B("pz", h)[:], True, True, "pD", 128, r=[W("BOf"), x("pz")], f32=True, name="zm")
            tt(T.ZQ[:, S(h)], T.QM[:, S(h)], zm, OP.mult, 128, r=[W("QM")], w=[hr("ZQ")], pr=["pD"], name="ZQ")
            cpv(T.ZU[:, S(h)], zm, 128, w=[hr("ZU")], pr=["pD"], name="ZU")
            vop(lambda v, h=h: v.tensor_tensor_scan(T.ZS[:, S(h)], T.NF[:], T.ZQ[:, S(h)], 0.0, OP.mult, OP.add), 128, r=[W("NF"), hr("ZQ")], w=[hr("ZS")], name="ZS")
            zl = ("ZL", 8 * h, 8 * h + 8)
            ts(T.ZL[:, 8 * h:8 * h + 8], T.ZS[:, 128 * h + 15:128 * h + 128:16], -1.0, OP.add, 8, r=[hr("ZS")], w=[zl], s2=0.0, op1=OP.max, name="ZL")
            mm(T.pD[:, :, 16 * h:16 * h + 16], T.BOf[:], B("pc", h)[:], True, True, "pD", 128, r=[x("pc")], f32=True, name="csv")
            flex(B("OC", h)[:], T.O[:].indirect(T.ZL[:, 8 * h:8 * h + 8]), 128, r=[W("O"), zl], w=[x("OC")], cyc=GCY, name="OC", only="S")
            vop(lambda v, h=h, VR=VR: v.tensor_tensor(B("OE", h)[:], T.O[:].indirect(T.ZL[:, 8 * h:8 * h + 8]), VR[:, S(h)], OP.is_equal), 128, r=[W("O"), zl, W("VR%d" % t)], w=[x("OE")], two=GCY, name="OE")
            tt(C[:, :, 48:64], T.oK[:, S(h)], C[:, :, 0:16], OP.mult, 128, r=[hr("oK")], pr=[ck], pw=[ck], name="hb")
        for h in H:
            x = lambda n: W(n + str(h)); hr = lambda n: (n, 128 * h, 128 * h + 128)
            n1 = T.pD[:, :, 16 * h:16 * h + 16]
            tt(n1, B("OE", h)[:], n1, OP.mult, 128, r=[x("OE")], pr=["pD"], pw=["pD"], name="n1")
            tt(T.NC[:, S(h)], B("OC", h)[:], n1, OP.add, 128, r=[x("OC")], w=[hr("NC")], pr=["pD"], name="NC")
        def de(u, a, z):
            ts(T.DE[:, 256 * u + a:256 * u + z], T.ZU[:, a:z], T.ZS[:, 16 * u + 15:16 * u + 16], OP.is_equal, z - a,
               r=[("ZU", a, z), ("ZS", 16 * u, 16 * u + 16)], w=[("DE", 256 * u + a, 256 * u + z)], two=0.5, name="DE")

        def dup(h, u, a, z, wt, stop=False):
            mm(T.pE[:, a:z], T[wt][:], T.DE[:, 256 * u + a:256 * u + z], False, stop, "pE", z - a, r=[("DE", 256 * u + a, 256 * u + z), W(wt)], name="DUP%d" % h)
        for h in H:
            hr = ("oK", 128 * h, 128 * h + 128)
            mm(T.pE[:, S(h)], T.Ib[:], T.DC[:, S(h)], True, False, "pE", 128, r=[W("Ib"), W("DC")], name="DUP%d" % h)
            mm(T.pE[:, S(h)], T.Ib[:], T.C128[:, S(h)], False, False, "pE", 128, r=[W("C128")], name="DUP%d" % h)
            mm(T.pE[:, S(h)], T.BN[:], T.oK[:, S(h)], False, False, "pE", 128, r=[W("BN"), hr], name="DUP%d" % h)
            for u in range(8 * h + 8):
                if u < 8 * h:
                    de(u, 128, 256)
                    dup(h, u, 128, 256, "L4")
                    continue
                de(u, 16 * u, 128 * h + 128)
                if u < 8 * h + 7: dup(h, u, 16 * u + 16, 128 * h + 128, "L4")
                dup(h, u, 16 * u, 16 * u + 16, "LW", u == 8 * h + 7)
        vop(lambda v: v.tensor_scalar(T.pE[:, 0:256], T.pE[:, 0:256], 0.0, 8192.0, OP.is_ge, OP.mult), 256, pr=["pE"], pw=["pE"], name="nlq")
        tt(T.fz[:], T.ZQ[:], T.pE[:, 0:256], OP.max, 256, r=[W("ZQ")], w=[W("fz")], pr=["pE"], name="fz")
        for h in H:
            vop(lambda v, h=h: v.tensor_tensor_scan(T.FS[:, S(h)], T.NF[:], T.fz[:, S(h)], 0.0, OP.mult, OP.add), 128, r=[W("NF"), ("fz", 128 * h, 128 * h + 128)], w=[("FS", 128 * h, 128 * h + 128)], name="FS")
        tt(T.fl[:], T.FS[:, 15::16], T.DL[:], OP.min, 16, r=[W("FS"), W("DL")], w=[W("fl")], name="fl")
        ts(T.FZ[:], T.fl[:], -1.0, OP.add, 16, r=[W("fl")], w=[W("FZ")], name="FZ")
        vop(lambda v: v.tensor_copy(T.O[:].indirect(T.FZ[:]), T.NC[:]), 256, r=[W("NC"), W("FZ")], w=[W("O")], two=3.0, name="scatter")
        G["wr"]["O"] = [y for y in G["wr"]["O"]]
        for h in H:
            hr = lambda n: (n, 128 * h, 128 * h + 128)
            ck = "pC%d" % h
            tt(T.XO[:, S(h)], T.O[:, hs(h)], P("C", h)[:, :, 32:48], OP.mult, 128, r=[oreg(h)], w=[hr("XO")], pr=[ck], name="XO")
            tt(T.O[:, hs(h)], T.XO[:, S(h)], P("C", h)[:, :, 48:64], OP.add, 128, r=[hr("XO")], w=[("O", 1536 * h, 1536 * h + 1536)], pr=[ck], name="O")
        for h in H:
            x = lambda n: W(n + str(h)); ck = "pA%d" % h; C = P("A", h)
            cr = lambda n: (n, 96 * h, 96 * h + 96)
            tt(T.CLk[:, 96 * h:96 * h + 96], T.CLf[:, 96 * h:96 * h + 96], T.KP[:, t], OP.mult, 96, r=[cr("CLf"), W("KP%d" % t)], w=[cr("CLk")], name="CLk")
            tt(B("BDc", h)[:], B("nC", h)[:], T.PM[:, t], OP.mult, 128, r=[x("nC"), W("PM%d" % t)], w=[x("BDc")], name="BDc")
            mm(C[:, :, 0:12], T.If[:], T.CLk[:, 96 * h:96 * h + 96], True, False, ck, 96, r=[cr("CLk"), W("If")], f32=True, name="CLp")
            mm(C[:, :, 0:12], B("BDc", h)[:], T.U4[:], False, True, ck, 96, r=[x("BDc"), W("U4")], f32=True, name="CLp")
            if not last: cpv(T.CLu[:, 96 * h:96 * h + 96], C[:, :, 0:12], 96, w=[cr("CLu")], pr=[ck], name="CLu")
            act(T.CLf[:, 96 * h:96 * h + 96], C[:, :, 0:12], 96, w=[cr("CLf")], pr=[ck], name="CLf")
        if last: break
        for h in H:
            mm(T.pA1[:, :, 58], T.ONE[:], B("win", h)[:, 0::16], h == 0, h == 1, "pA1", 8, r=[W("win%d" % h), W("ONE")], name="ZC")
        vop(lambda v: v.tensor_reduce(T.zr[:, 0:1], T.pA1[:, :, 58], AxisListType.X, OP.add), 8, w=[("zr", 0, 1)], pr=["pA1"], name="zr")
        cpv(T.zi[:, 0:1], T.zr[:, 0:1], 1, r=[("zr", 0, 1)], w=[("zi", 0, 1)])
        ts(T.zi[:, 1:2], T.zi[:, 0:1], 1, OP.bitwise_and, 1, r=[("zi", 0, 1)], w=[("zi", 1, 2)])
        ts(T.Zc[:], T.zi[:, 1:2], 9.0, OP.add, 1, r=[("zi", 1, 2)], w=[W("Zc")], name="Zc")
        for qi, q in enumerate(ds):
            s = (rank + q) % NR; ln = "L%d_%d" % (t + 1, s)
            arrive(s, t + 1, sa if qi == 0 else sb_, 8)
            for h in H:
                A = P("A", h); ak = "pA%d" % h
                flex(B("HLz", h)[:, :, 0:2], LU(t + 1, s)[:, h], 16, r=[W(ln)], w=[W("HLz%d" % h)], name="HLz")
                mm(A[:, :, 40:56], B("HLz", h)[:], T.Ib[:], True, True, ak, 128, r=[W("HLz%d" % h)], name="HLr")
                flex(T["WC%d" % q][:, hs(h)], A[:, :, 40:56], 128, w=[("WC%d" % q, 1536 * h, 1536 * h + 1536)], pr=[ak], name="WCu")
    vop(lambda v: v.transpose(T.TF[:], T.CLf[:]), 192, r=[W("CLf")], w=[W("TF")], name="yc")
    for e in range(2):
        for b in range(6):
            dma(T.yc[e::2, 512 * b:512 * b + 512], T.TF[:, 32 * b + 16 * e:32 * b + 16 * e + 16], 8, r=[W("TF")], name="st yc")
    dma(T.yo[:, 0:1536], T.O[:, 0:1536], 786, r=[("O", 0, 1536)], name="st yo")
    dma(T.yo[:, 1536:3072], T.O[:, 1536:3072], 786, r=[("O", 1536, 3072)], q="S", name="st yo")
    return G


ORDER = {}


def rank_program(g, core, T, topo):
    rank = T.rank_of(core)
    if rank is None:
        return
    G = build(core, T, topo, rank)
    if "o" not in ORDER: ORDER["o"] = schedule(G)
    order, eng, fin, st = ORDER["o"]
    Q = {"V": g.vector, "S": g.scalar, "P": g.tensor, "G": g, "Y": g.sync}
    ops = G["ops"]
    count = {}; known = {"V": {}, "S": {}, "P": {}, "G": {}, "Y": {}}; done = [None] * len(ops); clock = [None] * len(ops)
    for i in order:
        o = ops[i]; e = eng[i]
        if e not in Q:
            done[i] = (o["key"], o["cnt"]); clock[i] = {}
            continue
        kn = known[e]
        need = {}
        for j, raw in o["deps"].items():
            if eng[j] == e and not raw: continue
            k, c = done[j]
            if kn.get(k, 0) < c: need[k] = max(need.get(k, 0), c)
        cand = sorted(need.items())
        for j in o["deps"]:
            if eng[j] == e and not o["deps"][j]: continue
        for k, c in cand:
            if kn.get(k, 0) >= c: continue
            Q[e].wait_ge(T.sem[k], c)
            kn[k] = max(kn.get(k, 0), c)
            for j in o["deps"]:
                if done[j] == (k, c):
                    for kk, vv in clock[j].items(): kn[kk] = max(kn.get(kk, 0), vv)
        ins = o["fn"](Q, e)
        if o["key"] is None:
            k = "c" + e
            count[k] = count.get(k, 0) + 1
            ins.then_inc(T.sem[k], 1)
            done[i] = (k, count[k])
        else:
            k = o["key"]
            count[k] = count.get(k, 0) + o["cnt"]
            done[i] = (k, count[k])
        c = dict(kn); c[done[i][0]] = max(c.get(done[i][0], 0), done[i][1])
        clock[i] = c
    for k in sorted(count): g.wait_ge(T.sem[k], count[k])
